import numpy as np
import ml_dtypes


def mxq(x, axis, fmt="e4m3"):
    dtype, down = {"e4m3": (ml_dtypes.float8_e4m3fn, 7), "e5m2": (ml_dtypes.float8_e5m2, 14)}[fmt]
    v = np.moveaxis(np.asarray(x, np.float32).astype(ml_dtypes.bfloat16).astype(np.float64), axis, -1)
    blocks = v.reshape(v.shape[:-1] + (-1, 32))
    amax = np.abs(blocks).max(-1, keepdims=True)
    byte = np.maximum(np.where(amax > 0, np.frexp(amax)[1] - 1 + 127, 0) - down, 1)
    scale = np.exp2(byte - 127.0)
    codes = (blocks / scale).astype(np.float32).astype(dtype).astype(np.float64)
    return np.moveaxis((codes * scale).reshape(v.shape), -1, axis)


WIDE = False


def mx_kscale(k):
    if not WIDE:
        return np.ones(k)
    levels = np.array([10, -10, 5, -5, 0])
    if k % 512:
        return np.exp2(np.random.permutation(np.resize(levels, k // 32))).repeat(32)
    a = np.empty((k // 512, 16))
    for p in range(k // 512):
        a[p, :8] = np.random.permutation(np.resize(levels, 8))
        for g in range(8):
            far = levels[np.abs(levels - a[p, g]) >= 10]
            a[p, g + 8] = far[np.random.randint(len(far))]
    return np.exp2(a.ravel()).repeat(32)


def f64(x):
    return np.asarray(x).astype(np.float64)


def striped(idx):
    return np.tile(idx.reshape(-1, 16).T, (8, 1)).astype(np.uint16)


def unstriped(offs):
    return offs[:16].T.reshape(-1).astype(np.int64)


E2M1 = np.array([0.0, 0.5, 1.0, 1.5, 2.0, 3.0, 4.0, 6.0, -0.0, -0.5, -1.0, -1.5, -2.0, -3.0, -4.0, -6.0])


def pack_fp4(w):
    k, n = w.shape
    w = f64(np.asarray(w, np.float32).astype(ml_dtypes.bfloat16)).reshape(k // 32, 32, n)
    amax = np.abs(w).max(1)
    mant, ex = np.frexp(amax / 6.0)
    byte = np.clip(np.where(amax > 0, np.where(mant > 0.5, ex, ex - 1) + 127, 1), 1, 254)
    scaled = (w * np.exp2(127.0 - byte)[:, None, :]).reshape(k, n).astype(np.float32)
    c = np.ascontiguousarray(scaled.reshape(k // 512, 128, 4, n).transpose(0, 1, 3, 2)).astype(ml_dtypes.float4_e2m1fn).view(np.uint8) & 0xF
    words = (c[..., 0::2] | (c[..., 1::2] << 4)).reshape(k // 512, 128, 2 * n)
    return np.ascontiguousarray(words), np.ascontiguousarray(byte.astype(np.uint8).reshape(k // 512, 16, n))


def unpack_fp4(words, scales):
    g, _, n = scales.shape
    words = np.ascontiguousarray(words).reshape(g, 128, n, 2)
    nib = np.empty((g, 128, n, 4), np.uint8)
    nib[..., 0::2] = words & 0xF
    nib[..., 1::2] = words >> 4
    vals = E2M1[nib] * np.repeat(np.exp2(scales.astype(np.float64) - 127.0), 8, axis=1)[..., None]
    return vals.transpose(0, 1, 3, 2).reshape(g * 512, n)


def sigmoid(v):
    return 1.0 / (1.0 + np.exp(-np.maximum(v, -700.0)))


K, T, S, N, U = 1024, 2048, 1024, 128, 2048


def setup_inputs():
    n = np.random.standard_normal
    s = mx_kscale(K)[:, None]
    packed_w1 = pack_fp4(n((K, N)) / np.sqrt(K) / s)
    return {
        "xT": (n((K, T)) * s).astype(np.float32),
        "mem": n((N, U)).astype(np.float32),
        "w1_words": packed_w1[0],
        "w1_scales": packed_w1[1],
        "offs": striped(np.random.permutation(T)[:S]),
        "slot": striped(np.random.permutation(U)[:S]),
    }


def reference(xT, mem, w1_words, w1_scales, offs, slot):
    xq = mxq(f64(xT)[:, unstriped(offs)], 0, "e4m3")
    y = unpack_fp4(w1_words, w1_scales).T @ xq
    out = f64(mem).copy()
    out[:, unstriped(slot)] = f64(mem)[:, unstriped(slot)] * sigmoid(y)
    return out

@@ -1,0 +1,173 @@
+from contextlib import ExitStack
+
+import concourse.mybir as mybir
+
+K, T, S, N, U = 1024, 2048, 1024, 128, 2048
+FLOPS = 2 * K * N * S
+
+F32 = mybir.dt.float32
+BF16 = mybir.dt.bfloat16
+U32 = mybir.dt.uint32
+I32 = mybir.dt.int32
+U16 = mybir.dt.uint16
+U8 = mybir.dt.uint8
+FP8X4 = mybir.dt.float8_e4m3fn_x4
+FP4X4 = mybir.dt.float4_e2m1fn_x4
+SIGMOID = mybir.ActivationFunctionType.Sigmoid
+MULT = mybir.AluOpType.mult
+
+P = 128
+PASSES = K // 512
+HALF = T // 2
+VECTOR_COLS = (768, 768, 768, 704)
+OVERLAP = 16
+STRIDE = T - OVERLAP
+SLICE = 256
+GROUP = 128
+
+
+def tile_picked_idxput_gate_e_kernel(tc, xT, mem, w1_words, w1_scales, offs, slot, out):
+    nc = tc.nc
+    with ExitStack() as ctx:
+        keep = ctx.enter_context(tc.tile_pool(name="keep", bufs=1))
+        psum = ctx.enter_context(tc.psum_pool(name="psum", bufs=1))
+
+        store = keep.tile([P, U], F32, name="store")
+        slot_sb = keep.tile([P, S // 16], U16, name="slot_sb")
+        offs_sb = keep.tile([P, S // 16], U16, name="offs_sb")
+        w_words = keep.tile([P, PASSES, 2 * N], U8, name="w_words", align_bytes=64)
+        w_scales = keep.tile([P, PASSES, N], U8, name="w_scales", align_bytes=64)
+
+        warm_in = keep.tile([P, 1], F32, name="warm_in")
+        warm_out = keep.tile([P, 1], F32, name="warm_out")
+        nc.vector.memset(warm_in[:], 0.0)
+        nc.scalar.activation(warm_out[:], warm_in[:], SIGMOID)
+
+        nc.vector.memset(w_scales[:].bitcast(I32), 0)
+        for q in range(4):
+            nc.scalar.dma_start(
+                out=w_scales[32 * q : 32 * q + 4, :, :].bitcast(I32),
+                in_=w1_scales[:, 4 * q : 4 * q + 4, :].rearrange("z r c -> r z c").bitcast(I32),
+            )
+
+        x_rows = xT.rearrange("(z p u e) t -> z u p e t", z=PASSES, u=2, e=2)
+        raw = {}
+        for z in range(PASSES):
+            for u in range(2):
+                for h in (1, 0):
+                    raw[z, u, h] = keep.tile([P, 2, HALF], F32, name="raw%d%d%d" % (z, u, h))
+                    nc.sync.dma_start(out=raw[z, u, h][:], in_=x_rows[z, u, :, :, h * HALF : (h + 1) * HALF])
+                    if (z, u, h) == (0, 0, 1):
+                        nc.sync.dma_start(offs_sb[:], offs)
+                if (z, u) == (0, 1):
+                    nc.sync.dma_start(slot_sb[:], slot)
+                    nc.sync.dma_start(out=store[:], in_=mem)
+                    nc.sync.dma_start(
+                        out=w_words[:].bitcast(I32), in_=w1_words.rearrange("z p c -> p z c").bitcast(I32)
+                    )
+
+        windows = keep.tile([P, 2 * (4 * STRIDE + OVERLAP)], BF16, name="windows", align_bytes=64)
+
+        def make_pairs(z, u):
+            base = 2 * (2 * z + u) * STRIDE
+            flat = windows[:, base : base + 2 * T]
+            pairs = flat.rearrange("p (t e) -> p t e", e=2)
+            cols = VECTOR_COLS[2 * z + u]
+            upper = raw[z, u, 1][:].rearrange("p e c -> p c e")
+            lower = raw[z, u, 0][:].rearrange("p e c -> p c e")
+            nc.scalar.copy(pairs[:, HALF:T, :], upper)
+            nc.vector.tensor_copy(pairs[:, 0:cols, :], lower[:, 0:cols, :])
+            nc.scalar.copy(pairs[:, cols:HALF, :], lower[:, cols:HALF, :])
+            return flat.bitcast(U32)
+
+        acc = [psum.tile([P, GROUP], F32, name="acc%d" % g) for g in range(S // GROUP)]
+
+        def product(z, codes, scales, g, col):
+            nc.tensor.matmul_mx(
+                out=acc[g][:],
+                lhsT=w_words[:, z, :].bitcast(FP4X4),
+                lhsT_scale=w_scales[:, z, :],
+                rhs=codes[:, col : col + GROUP].bitcast(FP8X4),
+                rhs_scale=scales[:, col : col + GROUP],
+                start=(z == 0),
+                stop=(z == PASSES - 1),
+            )
+
+        def quantize(woven, width, label):
+            codes = keep.tile([P, width], U32, name="codes" + label, align_bytes=64)
+            scales = keep.tile([P, width], U8, name="scales" + label, align_bytes=64)
+            nc.vector.quantize_mx(out=codes[:].bitcast(FP8X4), scales=scales[:], in_=woven[:])
+            return codes, scales
+
+        def as_words(woven, dtype):
+            return woven[:].bitcast(dtype).rearrange("p (n u) -> p n u", u=2)
+
+        def entries(index_tile, a, b):
+            return index_tile[:, a // 16 : b // 16]
+
+        half = S // 2
+        picked0 = keep.tile([P, 2, S], U32, name="picked0")
+        window = make_pairs(0, 0)
+        nc.vector.tensor_copy(picked0[:, 0, :], window.indirect(offs_sb[:]))
+        window = make_pairs(0, 1)
+        woven0 = []
+        for h in range(2):
+            a, b = h * half, (h + 1) * half
+            nc.vector.tensor_copy(picked0[:, 1, a:b], window.indirect(entries(offs_sb, a, b)))
+            woven0.append(keep.tile([P, 4 * half], BF16, name="woven0_%d" % h, align_bytes=64))
+            nc.scalar.copy(as_words(woven0[h], U32), picked0[:, :, a:b].rearrange("p u n -> p n u"))
+        old = keep.tile([P, S], F32, name="old")
+        nc.vector.tensor_copy(old[:], store[:].indirect(slot_sb[:]))
+        for h in range(2):
+            codes, scales = quantize(woven0[h], half, "0_%d" % h)
+            for g in range(half // GROUP):
+                product(0, codes, scales, h * half // GROUP + g, g * GROUP)
+
+        slices = range(S // SLICE)
+        woven1 = [keep.tile([P, 4 * SLICE], BF16, name="woven1_%d" % s, align_bytes=64) for s in slices]
+        picked1 = {s: keep.tile([P, 2, SLICE], U32, name="picked1_%d" % s) for s in slices if s > 0}
+
+        def pick(window, u, s):
+            target = as_words(woven1[0], U32)[:, :, u] if s == 0 else picked1[s][:, u, :]
+            nc.vector.tensor_copy(target, window.indirect(entries(offs_sb, s * SLICE, (s + 1) * SLICE)))
+
+        window = make_pairs(1, 0)
+        for s in slices:
+            pick(window, 0, s)
+
+        window = make_pairs(1, 1)
+        puts = ((0, SLICE), (SLICE, 2 * SLICE), (2 * SLICE, S))
+        gates = {a: keep.tile([P, b - a], F32, name="gate%d" % a) for a, b in puts}
+
+        def gate(a, b):
+            first = max(start for start in gates if start <= a)
+            return gates[first][:, a - first : b - first]
+
+        def finish(s):
+            codes, scales = quantize(woven1[s], SLICE, "1_%d" % s)
+            for j in range(SLICE // GROUP):
+                g = s * (SLICE // GROUP) + j
+                product(1, codes, scales, g, j * GROUP)
+                nc.scalar.activation(gate(g * GROUP, (g + 1) * GROUP), acc[g][:], SIGMOID)
+
+        def weave(s):
+            nc.scalar.copy(as_words(woven1[s], U32), picked1[s][:].rearrange("p u n -> p n u"))
+
+        def put(a, b):
+            nc.vector.tensor_tensor(store[:].indirect(entries(slot_sb, a, b)), old[:, a:b], gate(a, b), MULT)
+
+        pick(window, 1, 0)
+        pick(window, 1, 1)
+        weave(1)
+        finish(0)
+        for s in (2, 3):
+            pick(window, 1, s)
+            weave(s)
+        finish(1)
+        put(*puts[0])
+        finish(2)
+        finish(3)
+        put(*puts[1])
+        put(*puts[2])
+
+        nc.sync.dma_start(out=out, in_=store[:])

@@ -18,11 +18,17 @@ MULT = mybir.AluOpType.mult
 
 P = 128
 PASSES = K // 512
-HALF = T // 2
-VECTOR_COLS = (768, 768, 768, 704)
+LOADS = (
+    ((0, 2048),),
+    ((1024, 2048), (0, 1024)),
+    ((1024, 2048), (0, 1024)),
+    ((1280, 2048), (512, 1280), (0, 512)),
+)
+VECTOR_COLS = (1344, 768, 768, 512)
 OVERLAP = 16
 STRIDE = T - OVERLAP
 SLICE = 256
+WOVEN_LATER = (1, 2)
 GROUP = 128
 
 
@@ -43,9 +49,9 @@ def tile_picked_idxput_gate_e_kernel(tc, xT, mem, w1_words, w1_scales, offs, slo
         nc.vector.memset(warm_in[:], 0.0)
         nc.scalar.activation(warm_out[:], warm_in[:], SIGMOID)
 
-        nc.vector.memset(w_scales[:].bitcast(I32), 0)
+        nc.gpsimd.memset(w_scales[:].bitcast(I32), 0)
         for q in range(4):
-            nc.scalar.dma_start(
+            nc.gpsimd.dma_start(
                 out=w_scales[32 * q : 32 * q + 4, :, :].bitcast(I32),
                 in_=w1_scales[:, 4 * q : 4 * q + 4, :].rearrange("z r c -> r z c").bitcast(I32),
             )
@@ -54,11 +60,12 @@ def tile_picked_idxput_gate_e_kernel(tc, xT, mem, w1_words, w1_scales, offs, slo
         raw = {}
         for z in range(PASSES):
             for u in range(2):
-                for h in (1, 0):
-                    raw[z, u, h] = keep.tile([P, 2, HALF], F32, name="raw%d%d%d" % (z, u, h))
-                    nc.sync.dma_start(out=raw[z, u, h][:], in_=x_rows[z, u, :, :, h * HALF : (h + 1) * HALF])
-                    if (z, u, h) == (0, 0, 1):
-                        nc.sync.dma_start(offs_sb[:], offs)
+                for a, b in LOADS[2 * z + u]:
+                    label = "raw%d%d_%d" % (z, u, a)
+                    raw[z, u, a] = keep.tile([P, 2, b - a], F32, name=label)
+                    nc.sync.dma_start(out=raw[z, u, a][:], in_=x_rows[z, u, :, :, a:b])
+                if (z, u) == (0, 0):
+                    nc.sync.dma_start(offs_sb[:], offs)
                 if (z, u) == (0, 1):
                     nc.sync.dma_start(slot_sb[:], slot)
                     nc.sync.dma_start(out=store[:], in_=mem)
@@ -73,11 +80,13 @@ def tile_picked_idxput_gate_e_kernel(tc, xT, mem, w1_words, w1_scales, offs, slo
             flat = windows[:, base : base + 2 * T]
             pairs = flat.rearrange("p (t e) -> p t e", e=2)
             cols = VECTOR_COLS[2 * z + u]
-            upper = raw[z, u, 1][:].rearrange("p e c -> p c e")
-            lower = raw[z, u, 0][:].rearrange("p e c -> p c e")
-            nc.scalar.copy(pairs[:, HALF:T, :], upper)
-            nc.vector.tensor_copy(pairs[:, 0:cols, :], lower[:, 0:cols, :])
-            nc.scalar.copy(pairs[:, cols:HALF, :], lower[:, cols:HALF, :])
+            for a, b in LOADS[2 * z + u]:
+                rows = raw[z, u, a][:].rearrange("p e c -> p c e")
+                if a < cols:
+                    nc.vector.tensor_copy(pairs[:, a:cols, :], rows[:, 0 : cols - a, :])
+                if b > cols:
+                    first = max(a, cols)
+                    nc.scalar.copy(pairs[:, first:b, :], rows[:, first - a : b - a, :])
             return flat.bitcast(U32)
 
         acc = [psum.tile([P, GROUP], F32, name="acc%d" % g) for g in range(S // GROUP)]
@@ -96,7 +105,7 @@ def tile_picked_idxput_gate_e_kernel(tc, xT, mem, w1_words, w1_scales, offs, slo
         def quantize(woven, width, label):
             codes = keep.tile([P, width], U32, name="codes" + label, align_bytes=64)
             scales = keep.tile([P, width], U8, name="scales" + label, align_bytes=64)
-            nc.vector.quantize_mx(out=codes[:].bitcast(FP8X4), scales=scales[:], in_=woven[:])
+            nc.vector.quantize_mx(out=codes[:].bitcast(FP8X4), scales=scales[:], in_=woven)
             return codes, scales
 
         def as_words(woven, dtype):
@@ -110,25 +119,23 @@ def tile_picked_idxput_gate_e_kernel(tc, xT, mem, w1_words, w1_scales, offs, slo
         window = make_pairs(0, 0)
         nc.vector.tensor_copy(picked0[:, 0, :], window.indirect(offs_sb[:]))
         window = make_pairs(0, 1)
-        woven0 = []
+        woven0 = keep.tile([P, 4 * S], BF16, name="woven0", align_bytes=64)
         for h in range(2):
             a, b = h * half, (h + 1) * half
             nc.vector.tensor_copy(picked0[:, 1, a:b], window.indirect(entries(offs_sb, a, b)))
-            woven0.append(keep.tile([P, 4 * half], BF16, name="woven0_%d" % h, align_bytes=64))
-            nc.scalar.copy(as_words(woven0[h], U32), picked0[:, :, a:b].rearrange("p u n -> p n u"))
+            nc.scalar.copy(as_words(woven0, U32)[:, a:b, :], picked0[:, :, a:b].rearrange("p u n -> p n u"))
         old = keep.tile([P, S], F32, name="old")
         nc.vector.tensor_copy(old[:], store[:].indirect(slot_sb[:]))
-        for h in range(2):
-            codes, scales = quantize(woven0[h], half, "0_%d" % h)
-            for g in range(half // GROUP):
-                product(0, codes, scales, h * half // GROUP + g, g * GROUP)
+        codes, scales = quantize(woven0[:], S, "0")
+        for g in range(S // GROUP):
+            product(0, codes, scales, g, g * GROUP)
 
         slices = range(S // SLICE)
         woven1 = [keep.tile([P, 4 * SLICE], BF16, name="woven1_%d" % s, align_bytes=64) for s in slices]
-        picked1 = {s: keep.tile([P, 2, SLICE], U32, name="picked1_%d" % s) for s in slices if s > 0}
+        picked1 = {s: keep.tile([P, 2, SLICE], U32, name="picked1_%d" % s) for s in WOVEN_LATER}
 
         def pick(window, u, s):
-            target = as_words(woven1[0], U32)[:, :, u] if s == 0 else picked1[s][:, u, :]
+            target = picked1[s][:, u, :] if s in WOVEN_LATER else as_words(woven1[s], U32)[:, :, u]
             nc.vector.tensor_copy(target, window.indirect(entries(offs_sb, s * SLICE, (s + 1) * SLICE)))
 
         window = make_pairs(1, 0)
@@ -136,18 +143,21 @@ def tile_picked_idxput_gate_e_kernel(tc, xT, mem, w1_words, w1_scales, offs, slo
             pick(window, 0, s)
 
         window = make_pairs(1, 1)
-        puts = ((0, SLICE), (SLICE, 2 * SLICE), (2 * SLICE, S))
+        puts = ((0, SLICE), (3 * SLICE, S), (SLICE, 3 * SLICE))
         gates = {a: keep.tile([P, b - a], F32, name="gate%d" % a) for a, b in puts}
 
         def gate(a, b):
             first = max(start for start in gates if start <= a)
             return gates[first][:, a - first : b - first]
 
-        def finish(s):
-            codes, scales = quantize(woven1[s], SLICE, "1_%d" % s)
+        def second_pass(s):
+            codes, scales = quantize(woven1[s][:], SLICE, "1_%d" % s)
             for j in range(SLICE // GROUP):
                 g = s * (SLICE // GROUP) + j
                 product(1, codes, scales, g, j * GROUP)
+
+        def open_gates(s):
+            for g in range(s * SLICE // GROUP, (s + 1) * SLICE // GROUP):
                 nc.scalar.activation(gate(g * GROUP, (g + 1) * GROUP), acc[g][:], SIGMOID)
 
         def weave(s):
@@ -157,17 +167,16 @@ def tile_picked_idxput_gate_e_kernel(tc, xT, mem, w1_words, w1_scales, offs, slo
             nc.vector.tensor_tensor(store[:].indirect(entries(slot_sb, a, b)), old[:, a:b], gate(a, b), MULT)
 
         pick(window, 1, 0)
-        pick(window, 1, 1)
-        weave(1)
-        finish(0)
-        for s in (2, 3):
+        second_pass(0)
+        open_gates(0)
+        for s in (1, 2):
             pick(window, 1, s)
             weave(s)
-        finish(1)
-        put(*puts[0])
-        finish(2)
-        finish(3)
-        put(*puts[1])
-        put(*puts[2])
+        pick(window, 1, 3)
+        for s in (3, 1, 2):
+            second_pass(s)
+            open_gates(s)
+        for a, b in puts:
+            put(a, b)
 
         nc.sync.dma_start(out=out, in_=store[:])

@@ -28,7 +28,7 @@ VECTOR_COLS = (1344, 768, 768, 512)
 OVERLAP = 16
 STRIDE = T - OVERLAP
 SLICE = 256
-WOVEN_LATER = (1, 2)
+WOVEN_LATER = (0, 1, 2, 3)
 GROUP = 128
 
 
@@ -49,13 +49,6 @@ def tile_picked_idxput_gate_e_kernel(tc, xT, mem, w1_words, w1_scales, offs, slo
         nc.vector.memset(warm_in[:], 0.0)
         nc.scalar.activation(warm_out[:], warm_in[:], SIGMOID)
 
-        nc.gpsimd.memset(w_scales[:].bitcast(I32), 0)
-        for q in range(4):
-            nc.gpsimd.dma_start(
-                out=w_scales[32 * q : 32 * q + 4, :, :].bitcast(I32),
-                in_=w1_scales[:, 4 * q : 4 * q + 4, :].rearrange("z r c -> r z c").bitcast(I32),
-            )
-
         x_rows = xT.rearrange("(z p u e) t -> z u p e t", z=PASSES, u=2, e=2)
         raw = {}
         for z in range(PASSES):
@@ -69,9 +62,15 @@ def tile_picked_idxput_gate_e_kernel(tc, xT, mem, w1_words, w1_scales, offs, slo
                 if (z, u) == (0, 1):
                     nc.sync.dma_start(slot_sb[:], slot)
                     nc.sync.dma_start(out=store[:], in_=mem)
-                    nc.sync.dma_start(
-                        out=w_words[:].bitcast(I32), in_=w1_words.rearrange("z p c -> p z c").bitcast(I32)
-                    )
+
+        nc.sync.dma_start(out=w_words[:].bitcast(I32), in_=w1_words.rearrange("z p c -> p z c").bitcast(I32))
+        nc.vector.memset(w_scales[:].bitcast(I32), 0)
+        for q in range(4):
+            nc.sync.dma_start(
+                out=w_scales[32 * q : 32 * q + 4, :, :].bitcast(I32),
+                in_=w1_scales[:, 4 * q : 4 * q + 4, :].rearrange("z r c -> r z c").bitcast(I32),
+            )
+
 
         windows = keep.tile([P, 2 * (4 * STRIDE + OVERLAP)], BF16, name="windows", align_bytes=64)
 
@@ -143,7 +142,7 @@ def tile_picked_idxput_gate_e_kernel(tc, xT, mem, w1_words, w1_scales, offs, slo
             pick(window, 0, s)
 
         window = make_pairs(1, 1)
-        puts = ((0, SLICE), (3 * SLICE, S), (SLICE, 3 * SLICE))
+        puts = ((0, SLICE), (SLICE, S))
         gates = {a: keep.tile([P, b - a], F32, name="gate%d" % a) for a, b in puts}
 
         def gate(a, b):
@@ -166,14 +165,10 @@ def tile_picked_idxput_gate_e_kernel(tc, xT, mem, w1_words, w1_scales, offs, slo
         def put(a, b):
             nc.vector.tensor_tensor(store[:].indirect(entries(slot_sb, a, b)), old[:, a:b], gate(a, b), MULT)
 
-        pick(window, 1, 0)
-        second_pass(0)
-        open_gates(0)
-        for s in (1, 2):
+        for s in slices:
             pick(window, 1, s)
             weave(s)
-        pick(window, 1, 3)
-        for s in (3, 1, 2):
+        for s in slices:
             second_pass(s)
             open_gates(s)
         for a, b in puts:

@@ -14,22 +14,21 @@ U8 = mybir.dt.uint8
 FP8X4 = mybir.dt.float8_e4m3fn_x4
 FP4X4 = mybir.dt.float4_e2m1fn_x4
 SIGMOID = mybir.ActivationFunctionType.Sigmoid
+COPY = mybir.ActivationFunctionType.Copy
 MULT = mybir.AluOpType.mult
 
 P = 128
 PASSES = K // 512
 LOADS = (
-    ((0, 2048),),
-    ((1024, 2048), (0, 1024)),
-    ((1024, 2048), (0, 1024)),
-    ((1280, 2048), (512, 1280), (0, 512)),
+    ((0, 1024, 256), (1024, 2048, 704)),
+    ((0, 1024, 0), (1024, 2048, 704)),
+    ((0, 768, 0), (768, 1536, 0), (1536, 2048, 384)),
 )
-VECTOR_COLS = (1344, 768, 768, 512)
-OVERLAP = 16
-STRIDE = T - OVERLAP
+LAST_LOADS = ((0, 768), (768, 1536), (1536, 2048))
+HALF = S // 2
 SLICE = 256
-WOVEN_LATER = (0, 1, 2, 3)
 GROUP = 128
+PARTS = ((0, SLICE), (SLICE, S))
 
 
 def tile_picked_idxput_gate_e_kernel(tc, xT, mem, w1_words, w1_scales, offs, slot, out):
@@ -48,130 +47,108 @@ def tile_picked_idxput_gate_e_kernel(tc, xT, mem, w1_words, w1_scales, offs, slo
         warm_out = keep.tile([P, 1], F32, name="warm_out")
         nc.vector.memset(warm_in[:], 0.0)
         nc.scalar.activation(warm_out[:], warm_in[:], SIGMOID)
-
-        x_rows = xT.rearrange("(z p u e) t -> z u p e t", z=PASSES, u=2, e=2)
-        raw = {}
-        for z in range(PASSES):
-            for u in range(2):
-                for a, b in LOADS[2 * z + u]:
-                    label = "raw%d%d_%d" % (z, u, a)
-                    raw[z, u, a] = keep.tile([P, 2, b - a], F32, name=label)
-                    nc.sync.dma_start(out=raw[z, u, a][:], in_=x_rows[z, u, :, :, a:b])
-                if (z, u) == (0, 0):
-                    nc.sync.dma_start(offs_sb[:], offs)
-                if (z, u) == (0, 1):
-                    nc.sync.dma_start(slot_sb[:], slot)
-                    nc.sync.dma_start(out=store[:], in_=mem)
-
-        nc.sync.dma_start(out=w_words[:].bitcast(I32), in_=w1_words.rearrange("z p c -> p z c").bitcast(I32))
         nc.vector.memset(w_scales[:].bitcast(I32), 0)
+
+        x_pairs = xT.rearrange("(z p u e) t -> z u p e t", z=PASSES, u=2, e=2)
+        first_row = keep.tile([P, T], F32, name="first_row", align_bytes=64)
+        last_row = keep.tile([P, T], F32, name="last_row", align_bytes=64)
+        nc.sync.dma_start(out=first_row[:], in_=x_pairs[1, 1, :, 0, :])
+        nc.sync.dma_start(offs_sb[:], offs)
+        raw = {}
+        for pair in range(3):
+            for a, b, split in LOADS[pair]:
+                label = "raw%d_%d" % (pair, a)
+                raw[pair, a] = keep.tile([P, 2, b - a], F32, name=label, align_bytes=64)
+                nc.sync.dma_start(out=raw[pair, a][:], in_=x_pairs[pair // 2, pair % 2, :, :, a:b])
+            if pair == 0:
+                nc.sync.dma_start(slot_sb[:], slot)
+        for a, b in LAST_LOADS:
+            nc.sync.dma_start(out=last_row[:, a:b], in_=x_pairs[1, 1, :, 1, a:b])
+        nc.sync.dma_start(out=store[:], in_=mem)
+        nc.sync.dma_start(out=w_words[:].bitcast(I32), in_=w1_words.rearrange("z p c -> p z c").bitcast(I32))
         for q in range(4):
             nc.sync.dma_start(
                 out=w_scales[32 * q : 32 * q + 4, :, :].bitcast(I32),
                 in_=w1_scales[:, 4 * q : 4 * q + 4, :].rearrange("z r c -> r z c").bitcast(I32),
             )
 
-
-        windows = keep.tile([P, 2 * (4 * STRIDE + OVERLAP)], BF16, name="windows", align_bytes=64)
-
-        def make_pairs(z, u):
-            base = 2 * (2 * z + u) * STRIDE
-            flat = windows[:, base : base + 2 * T]
-            pairs = flat.rearrange("p (t e) -> p t e", e=2)
-            cols = VECTOR_COLS[2 * z + u]
-            for a, b in LOADS[2 * z + u]:
-                rows = raw[z, u, a][:].rearrange("p e c -> p c e")
-                if a < cols:
-                    nc.vector.tensor_copy(pairs[:, a:cols, :], rows[:, 0 : cols - a, :])
-                if b > cols:
-                    first = max(a, cols)
-                    nc.scalar.copy(pairs[:, first:b, :], rows[:, first - a : b - a, :])
-            return flat.bitcast(U32)
+        def make_pairs(pair):
+            label = "window%d" % pair
+            flat = keep.tile([P, 2 * T], BF16, name=label, align_bytes=64)
+            pairs = flat[:].rearrange("p (t e) -> p t e", e=2)
+            for a, b, split in LOADS[pair]:
+                rows = raw[pair, a][:].rearrange("p e c -> p c e")
+                if split > 0:
+                    nc.vector.tensor_copy(pairs[:, a : a + split, :], rows[:, 0:split, :])
+                if split < b - a:
+                    nc.scalar.copy(pairs[:, a + split : b, :], rows[:, split : b - a, :])
+            return flat[:].bitcast(U32)
 
         acc = [psum.tile([P, GROUP], F32, name="acc%d" % g) for g in range(S // GROUP)]
 
-        def product(z, codes, scales, g, col):
-            nc.tensor.matmul_mx(
-                out=acc[g][:],
-                lhsT=w_words[:, z, :].bitcast(FP4X4),
-                lhsT_scale=w_scales[:, z, :],
-                rhs=codes[:, col : col + GROUP].bitcast(FP8X4),
-                rhs_scale=scales[:, col : col + GROUP],
-                start=(z == 0),
-                stop=(z == PASSES - 1),
-            )
-
-        def quantize(woven, width, label):
-            codes = keep.tile([P, width], U32, name="codes" + label, align_bytes=64)
-            scales = keep.tile([P, width], U8, name="scales" + label, align_bytes=64)
+        def quantize_and_multiply(z, a, woven):
+            codes = keep.tile([P, SLICE], U32, name="codes%d_%d" % (z, a), tag="codes%d" % a, align_bytes=64)
+            scales = keep.tile([P, SLICE], U8, name="scales%d_%d" % (z, a), align_bytes=64)
             nc.vector.quantize_mx(out=codes[:].bitcast(FP8X4), scales=scales[:], in_=woven)
-            return codes, scales
-
-        def as_words(woven, dtype):
-            return woven[:].bitcast(dtype).rearrange("p (n u) -> p n u", u=2)
+            for col in range(0, SLICE, GROUP):
+                nc.tensor.matmul_mx(
+                    out=acc[(a + col) // GROUP][:],
+                    lhsT=w_words[:, z, :].bitcast(FP4X4),
+                    lhsT_scale=w_scales[:, z, :],
+                    rhs=codes[:, col : col + GROUP].bitcast(FP8X4),
+                    rhs_scale=scales[:, col : col + GROUP],
+                    start=(z == 0),
+                    stop=(z == PASSES - 1),
+                )
 
         def entries(index_tile, a, b):
             return index_tile[:, a // 16 : b // 16]
 
-        half = S // 2
-        picked0 = keep.tile([P, 2, S], U32, name="picked0")
-        window = make_pairs(0, 0)
-        nc.vector.tensor_copy(picked0[:, 0, :], window.indirect(offs_sb[:]))
-        window = make_pairs(0, 1)
+        def as_words(woven):
+            return woven[:].bitcast(U32).rearrange("p (n u) -> p n u", u=2)
+
         woven0 = keep.tile([P, 4 * S], BF16, name="woven0", align_bytes=64)
+        woven1 = {a: keep.tile([P, 4 * (b - a)], BF16, name="woven1_%d" % a, align_bytes=64) for a, b in PARTS}
+
+        def woven1_cols(a, b):
+            first = max(start for start in woven1 if start <= a)
+            return woven1[first][:, 4 * (a - first) : 4 * (b - first)]
+
+        def plane(a, b, t):
+            return woven1_cols(a, b).rearrange("p (n t) -> p n t", t=4)[:, :, t]
+
+        for a, b in PARTS:
+            nc.vector.tensor_copy(plane(a, b, 2), first_row[:].indirect(entries(offs_sb, a, b)))
+        window = make_pairs(0)
+        nc.vector.tensor_copy(as_words(woven0)[:, :, 0], window.indirect(offs_sb[:]))
+        window = make_pairs(1)
+        for a in (0, HALF):
+            nc.vector.tensor_copy(as_words(woven0)[:, a : a + HALF, 1], window.indirect(entries(offs_sb, a, a + HALF)))
+        for a in range(0, S, SLICE):
+            quantize_and_multiply(0, a, woven0[:, 4 * a : 4 * (a + SLICE)])
+        window = make_pairs(2)
+        for a, b in PARTS:
+            nc.vector.tensor_copy(as_words(woven1[a])[:, :, 0], window.indirect(entries(offs_sb, a, b)))
+
+        last_window = keep.tile([P, T], BF16, name="last_window", tag="first_row", align_bytes=64)
+        for a, b in LAST_LOADS:
+            nc.scalar.copy(last_window[:, a:b], last_row[:, a:b])
+        for a, b in ((0, SLICE), (SLICE, HALF), (HALF, S)):
+            nc.scalar.activation(plane(a, b, 3), last_window[:].indirect(entries(offs_sb, a, b)), COPY)
+
+        old = []
+        gates = []
+        for h, tag in enumerate(("old0", "woven1_0")):
+            old.append(keep.tile([P, HALF], F32, name="old%d" % h, tag=tag, align_bytes=64))
+            nc.vector.tensor_copy(old[h][:], store[:].indirect(entries(slot_sb, h * HALF, (h + 1) * HALF)))
+            for a in range(h * HALF, (h + 1) * HALF, SLICE):
+                quantize_and_multiply(1, a, woven1_cols(a, a + SLICE))
+            gates.append(keep.tile([P, HALF], F32, name="gate%d" % h))
+            for col in range(0, HALF, GROUP):
+                nc.scalar.activation(gates[h][:, col : col + GROUP], acc[(h * HALF + col) // GROUP][:], SIGMOID)
         for h in range(2):
-            a, b = h * half, (h + 1) * half
-            nc.vector.tensor_copy(picked0[:, 1, a:b], window.indirect(entries(offs_sb, a, b)))
-            nc.scalar.copy(as_words(woven0, U32)[:, a:b, :], picked0[:, :, a:b].rearrange("p u n -> p n u"))
-        old = keep.tile([P, S], F32, name="old")
-        nc.vector.tensor_copy(old[:], store[:].indirect(slot_sb[:]))
-        codes, scales = quantize(woven0[:], S, "0")
-        for g in range(S // GROUP):
-            product(0, codes, scales, g, g * GROUP)
-
-        slices = range(S // SLICE)
-        woven1 = [keep.tile([P, 4 * SLICE], BF16, name="woven1_%d" % s, align_bytes=64) for s in slices]
-        picked1 = {s: keep.tile([P, 2, SLICE], U32, name="picked1_%d" % s) for s in WOVEN_LATER}
-
-        def pick(window, u, s):
-            target = picked1[s][:, u, :] if s in WOVEN_LATER else as_words(woven1[s], U32)[:, :, u]
-            nc.vector.tensor_copy(target, window.indirect(entries(offs_sb, s * SLICE, (s + 1) * SLICE)))
-
-        window = make_pairs(1, 0)
-        for s in slices:
-            pick(window, 0, s)
-
-        window = make_pairs(1, 1)
-        puts = ((0, SLICE), (SLICE, S))
-        gates = {a: keep.tile([P, b - a], F32, name="gate%d" % a) for a, b in puts}
-
-        def gate(a, b):
-            first = max(start for start in gates if start <= a)
-            return gates[first][:, a - first : b - first]
-
-        def second_pass(s):
-            codes, scales = quantize(woven1[s][:], SLICE, "1_%d" % s)
-            for j in range(SLICE // GROUP):
-                g = s * (SLICE // GROUP) + j
-                product(1, codes, scales, g, j * GROUP)
-
-        def open_gates(s):
-            for g in range(s * SLICE // GROUP, (s + 1) * SLICE // GROUP):
-                nc.scalar.activation(gate(g * GROUP, (g + 1) * GROUP), acc[g][:], SIGMOID)
-
-        def weave(s):
-            nc.scalar.copy(as_words(woven1[s], U32), picked1[s][:].rearrange("p u n -> p n u"))
-
-        def put(a, b):
-            nc.vector.tensor_tensor(store[:].indirect(entries(slot_sb, a, b)), old[:, a:b], gate(a, b), MULT)
-
-        for s in slices:
-            pick(window, 1, s)
-            weave(s)
-        for s in slices:
-            second_pass(s)
-            open_gates(s)
-        for a, b in puts:
-            put(a, b)
+            nc.vector.tensor_tensor(
+                store[:].indirect(entries(slot_sb, h * HALF, (h + 1) * HALF)), old[h][:], gates[h][:], MULT
+            )
 
         nc.sync.dma_start(out=out, in_=store[:])

@@ -20,8 +20,8 @@ MULT = mybir.AluOpType.mult
 P = 128
 PASSES = K // 512
 LOADS = (
-    ((0, 1024, 256), (1024, 2048, 704)),
-    ((0, 1024, 0), (1024, 2048, 704)),
+    ((0, 1024, 640), (1024, 2048, 640)),
+    ((0, 1024, 0), (1024, 1664, 640), (1664, 2048, 256)),
     ((0, 768, 0), (768, 1536, 0), (1536, 2048, 384)),
 )
 LAST_LOADS = ((0, 768), (768, 1536), (1536, 2048))
@@ -54,14 +54,20 @@ def tile_picked_idxput_gate_e_kernel(tc, xT, mem, w1_words, w1_scales, offs, slo
         last_row = keep.tile([P, T], F32, name="last_row", align_bytes=64)
         nc.sync.dma_start(out=first_row[:], in_=x_pairs[1, 1, :, 0, :])
         nc.sync.dma_start(offs_sb[:], offs)
+        x_flat = xT.rearrange("(z p u e) t -> z u p (e t)", z=PASSES, u=2, e=2)
         raw = {}
-        for pair in range(3):
+        flat = keep.tile([P, 2 * T], F32, name="raw0", align_bytes=64)
+        done = 0
+        for a, b, split in LOADS[0]:
+            nc.sync.dma_start(out=flat[:, done : T + b], in_=x_flat[0, 0, :, done : T + b])
+            done = T + b
+            raw[0, a] = flat[:].rearrange("p (e c) -> p c e", e=2)[:, a:b, :]
+        nc.sync.dma_start(slot_sb[:], slot)
+        for pair in range(1, 3):
             for a, b, split in LOADS[pair]:
-                label = "raw%d_%d" % (pair, a)
-                raw[pair, a] = keep.tile([P, 2, b - a], F32, name=label, align_bytes=64)
-                nc.sync.dma_start(out=raw[pair, a][:], in_=x_pairs[pair // 2, pair % 2, :, :, a:b])
-            if pair == 0:
-                nc.sync.dma_start(slot_sb[:], slot)
+                piece = keep.tile([P, 2, b - a], F32, name="raw%d_%d" % (pair, a), align_bytes=64)
+                nc.sync.dma_start(out=piece[:], in_=x_pairs[pair // 2, pair % 2, :, :, a:b])
+                raw[pair, a] = piece[:].rearrange("p e c -> p c e")
         for a, b in LAST_LOADS:
             nc.sync.dma_start(out=last_row[:, a:b], in_=x_pairs[1, 1, :, 1, a:b])
         nc.sync.dma_start(out=store[:], in_=mem)
@@ -77,7 +83,7 @@ def tile_picked_idxput_gate_e_kernel(tc, xT, mem, w1_words, w1_scales, offs, slo
             flat = keep.tile([P, 2 * T], BF16, name=label, align_bytes=64)
             pairs = flat[:].rearrange("p (t e) -> p t e", e=2)
             for a, b, split in LOADS[pair]:
-                rows = raw[pair, a][:].rearrange("p e c -> p c e")
+                rows = raw[pair, a]
                 if split > 0:
                     nc.vector.tensor_copy(pairs[:, a : a + split, :], rows[:, 0:split, :])
                 if split < b - a:
@@ -107,7 +113,8 @@ def tile_picked_idxput_gate_e_kernel(tc, xT, mem, w1_words, w1_scales, offs, slo
         def as_words(woven):
             return woven[:].bitcast(U32).rearrange("p (n u) -> p n u", u=2)
 
-        woven0 = keep.tile([P, 4 * S], BF16, name="woven0", align_bytes=64)
+        picked0 = [keep.tile([P, 2, HALF], U32, name="picked0_%d" % h, align_bytes=64) for h in range(2)]
+        woven0 = [keep.tile([P, 4 * HALF], BF16, name="woven0_%d" % h, align_bytes=64) for h in range(2)]
         woven1 = {a: keep.tile([P, 4 * (b - a)], BF16, name="woven1_%d" % a, align_bytes=64) for a, b in PARTS}
 
         def woven1_cols(a, b):
@@ -119,13 +126,17 @@ def tile_picked_idxput_gate_e_kernel(tc, xT, mem, w1_words, w1_scales, offs, slo
 
         for a, b in PARTS:
             nc.vector.tensor_copy(plane(a, b, 2), first_row[:].indirect(entries(offs_sb, a, b)))
-        window = make_pairs(0)
-        nc.vector.tensor_copy(as_words(woven0)[:, :, 0], window.indirect(offs_sb[:]))
-        window = make_pairs(1)
-        for a in (0, HALF):
-            nc.vector.tensor_copy(as_words(woven0)[:, a : a + HALF, 1], window.indirect(entries(offs_sb, a, a + HALF)))
+        for u in range(2):
+            window = make_pairs(u)
+            for h in range(2):
+                nc.vector.tensor_copy(picked0[h][:, u, :], window.indirect(entries(offs_sb, h * HALF, (h + 1) * HALF)))
+        for h in range(2):
+            nc.vector.tensor_copy(
+                woven0[h][:].bitcast(I32).rearrange("p (n u) -> p n u", u=2),
+                picked0[h][:].bitcast(I32).rearrange("p u n -> p n u"),
+            )
         for a in range(0, S, SLICE):
-            quantize_and_multiply(0, a, woven0[:, 4 * a : 4 * (a + SLICE)])
+            quantize_and_multiply(0, a, woven0[a // HALF][:, 4 * (a % HALF) : 4 * (a % HALF + SLICE)])
         window = make_pairs(2)
         for a, b in PARTS:
             nc.vector.tensor_copy(as_words(woven1[a])[:, :, 0], window.indirect(entries(offs_sb, a, b)))

@@ -21,8 +21,8 @@ P = 128
 PASSES = K // 512
 LOADS = (
     ((0, 1024, 640), (1024, 2048, 640)),
-    ((0, 1024, 0), (1024, 1664, 640), (1664, 2048, 256)),
-    ((0, 768, 0), (768, 1536, 0), (1536, 2048, 384)),
+    ((0, 832, 0), (832, 1728, 576), (1728, 2048, 192)),
+    ((0, 512, 0), (512, 1024, 0), (1024, 1536, 0), (1536, 2048, 128)),
 )
 LAST_LOADS = ((0, 768), (768, 1536), (1536, 2048))
 HALF = S // 2

@@ -16,6 +16,7 @@ FP4X4 = mybir.dt.float4_e2m1fn_x4
 SIGMOID = mybir.ActivationFunctionType.Sigmoid
 COPY = mybir.ActivationFunctionType.Copy
 MULT = mybir.AluOpType.mult
+ADD = mybir.AluOpType.add
 
 P = 128
 PASSES = K // 512
@@ -24,7 +25,7 @@ LOADS = (
     ((0, 832, 0), (832, 1728, 576), (1728, 2048, 192)),
     ((0, 512, 0), (512, 1024, 0), (1024, 1536, 0), (1536, 2048, 128)),
 )
-LAST_LOADS = ((0, 768), (768, 1536), (1536, 2048))
+LAST_LOADS = ((0, 768, 768), (768, 1536, 0), (1536, 2048, 224))
 HALF = S // 2
 SLICE = 256
 GROUP = 128
@@ -68,7 +69,7 @@ def tile_picked_idxput_gate_e_kernel(tc, xT, mem, w1_words, w1_scales, offs, slo
                 piece = keep.tile([P, 2, b - a], F32, name="raw%d_%d" % (pair, a), align_bytes=64)
                 nc.sync.dma_start(out=piece[:], in_=x_pairs[pair // 2, pair % 2, :, :, a:b])
                 raw[pair, a] = piece[:].rearrange("p e c -> p c e")
-        for a, b in LAST_LOADS:
+        for a, b, split in LAST_LOADS:
             nc.sync.dma_start(out=last_row[:, a:b], in_=x_pairs[1, 1, :, 1, a:b])
         nc.sync.dma_start(out=store[:], in_=mem)
         nc.sync.dma_start(out=w_words[:].bitcast(I32), in_=w1_words.rearrange("z p c -> p z c").bitcast(I32))
@@ -141,9 +142,12 @@ def tile_picked_idxput_gate_e_kernel(tc, xT, mem, w1_words, w1_scales, offs, slo
         for a, b in PARTS:
             nc.vector.tensor_copy(as_words(woven1[a])[:, :, 0], window.indirect(entries(offs_sb, a, b)))
 
-        last_window = keep.tile([P, T], BF16, name="last_window", tag="first_row", align_bytes=64)
-        for a, b in LAST_LOADS:
-            nc.scalar.copy(last_window[:, a:b], last_row[:, a:b])
+        last_window = keep.tile([P, T], BF16, name="last_window", tag="raw2_1536", align_bytes=64)
+        for a, b, split in LAST_LOADS:
+            if split > 0:
+                nc.gpsimd.tensor_scalar(last_window[:, a : a + split], last_row[:, a : a + split], 1.0, 0.0, MULT, ADD)
+            if split < b - a:
+                nc.scalar.copy(last_window[:, a + split : b], last_row[:, a + split : b])
         for a, b in ((0, SLICE), (SLICE, HALF), (HALF, S)):
             nc.scalar.activation(plane(a, b, 3), last_window[:].indirect(entries(offs_sb, a, b)), COPY)
 

@@ -23,13 +23,13 @@ PASSES = K // 512
 LOADS = (
     ((0, 1024, 640), (1024, 2048, 640)),
     ((0, 832, 0), (832, 1728, 576), (1728, 2048, 192)),
-    ((0, 512, 0), (512, 1024, 0), (1024, 1536, 0), (1536, 2048, 128)),
+    ((0, 512, 0), (512, 1024, 0), (1024, 1536, 0), (1536, 2048, 256)),
 )
-LAST_LOADS = ((0, 768, 768), (768, 1536, 0), (1536, 2048, 224))
+LAST_LOADS = ((0, 768, 0), (768, 1536, 768), (1536, 2048, 0))
 HALF = S // 2
 SLICE = 256
 GROUP = 128
-PARTS = ((0, SLICE), (SLICE, S))
+PARTS = ((0, SLICE), (SLICE, HALF), (HALF, S))
 
 
 def tile_picked_idxput_gate_e_kernel(tc, xT, mem, w1_words, w1_scales, offs, slot, out):
@@ -87,17 +87,22 @@ def tile_picked_idxput_gate_e_kernel(tc, xT, mem, w1_words, w1_scales, offs, slo
                 rows = raw[pair, a]
                 if split > 0:
                     nc.vector.tensor_copy(pairs[:, a : a + split, :], rows[:, 0:split, :])
-                if split < b - a:
+                if (pair, a) == (2, 0):
+                    nc.gpsimd.tensor_scalar(pairs[:, a:b, :], rows, 1.0, 0.0, MULT, ADD)
+                elif split < b - a:
                     nc.scalar.copy(pairs[:, a + split : b, :], rows[:, split : b - a, :])
             return flat[:].bitcast(U32)
 
         acc = [psum.tile([P, GROUP], F32, name="acc%d" % g) for g in range(S // GROUP)]
 
-        def quantize_and_multiply(z, a, woven):
-            codes = keep.tile([P, SLICE], U32, name="codes%d_%d" % (z, a), tag="codes%d" % a, align_bytes=64)
-            scales = keep.tile([P, SLICE], U8, name="scales%d_%d" % (z, a), align_bytes=64)
+        def quantize(z, a, b, woven, tag):
+            codes = keep.tile([P, b - a], U32, name="codes%d_%d" % (z, a), tag=tag, align_bytes=64)
+            scales = keep.tile([P, b - a], U8, name="scales%d_%d" % (z, a), align_bytes=64)
             nc.vector.quantize_mx(out=codes[:].bitcast(FP8X4), scales=scales[:], in_=woven)
-            for col in range(0, SLICE, GROUP):
+            return codes, scales
+
+        def multiply(z, a, b, codes, scales):
+            for col in range(0, b - a, GROUP):
                 nc.tensor.matmul_mx(
                     out=acc[(a + col) // GROUP][:],
                     lhsT=w_words[:, z, :].bitcast(FP4X4),
@@ -136,34 +141,31 @@ def tile_picked_idxput_gate_e_kernel(tc, xT, mem, w1_words, w1_scales, offs, slo
                 woven0[h][:].bitcast(I32).rearrange("p (n u) -> p n u", u=2),
                 picked0[h][:].bitcast(I32).rearrange("p u n -> p n u"),
             )
-        for a in range(0, S, SLICE):
-            quantize_and_multiply(0, a, woven0[a // HALF][:, 4 * (a % HALF) : 4 * (a % HALF + SLICE)])
+        for a, b in PARTS:
+            woven = woven0[a // HALF][:, 4 * (a % HALF) : 4 * (a % HALF + b - a)]
+            multiply(0, a, b, *quantize(0, a, b, woven, "codes%d" % a))
         window = make_pairs(2)
         for a, b in PARTS:
             nc.vector.tensor_copy(as_words(woven1[a])[:, :, 0], window.indirect(entries(offs_sb, a, b)))
 
-        last_window = keep.tile([P, T], BF16, name="last_window", tag="raw2_1536", align_bytes=64)
+        last_window = keep.tile([P, T], BF16, name="last_window", tag="first_row", align_bytes=64)
         for a, b, split in LAST_LOADS:
             if split > 0:
                 nc.gpsimd.tensor_scalar(last_window[:, a : a + split], last_row[:, a : a + split], 1.0, 0.0, MULT, ADD)
             if split < b - a:
                 nc.scalar.copy(last_window[:, a + split : b], last_row[:, a + split : b])
-        for a, b in ((0, SLICE), (SLICE, HALF), (HALF, S)):
+        for a, b in PARTS:
             nc.scalar.activation(plane(a, b, 3), last_window[:].indirect(entries(offs_sb, a, b)), COPY)
 
-        old = []
-        gates = []
-        for h, tag in enumerate(("old0", "woven1_0")):
-            old.append(keep.tile([P, HALF], F32, name="old%d" % h, tag=tag, align_bytes=64))
-            nc.vector.tensor_copy(old[h][:], store[:].indirect(entries(slot_sb, h * HALF, (h + 1) * HALF)))
-            for a in range(h * HALF, (h + 1) * HALF, SLICE):
-                quantize_and_multiply(1, a, woven1_cols(a, a + SLICE))
-            gates.append(keep.tile([P, HALF], F32, name="gate%d" % h))
-            for col in range(0, HALF, GROUP):
-                nc.scalar.activation(gates[h][:, col : col + GROUP], acc[(h * HALF + col) // GROUP][:], SIGMOID)
-        for h in range(2):
-            nc.vector.tensor_tensor(
-                store[:].indirect(entries(slot_sb, h * HALF, (h + 1) * HALF)), old[h][:], gates[h][:], MULT
-            )
+        multiply(1, 0, SLICE, *quantize(1, 0, SLICE, woven1[0][:], "first"))
+        old = keep.tile([P, S], F32, name="old", tag="woven1_0", align_bytes=64)
+        nc.vector.tensor_copy(old[:], store[:].indirect(slot_sb[:]))
+        for a, b in PARTS[1:]:
+            multiply(1, a, b, *quantize(1, a, b, woven1[a][:], "codes%d" % a))
+        for a, b in ((0, SLICE), (SLICE, S)):
+            gate = keep.tile([P, b - a], F32, name="gate%d" % a)
+            for col in range(a, b, GROUP):
+                nc.scalar.activation(gate[:, col - a : col - a + GROUP], acc[col // GROUP][:], SIGMOID)
+            nc.vector.tensor_tensor(store[:].indirect(entries(slot_sb, a, b)), old[:, a:b], gate[:], MULT)
 
         nc.sync.dma_start(out=out, in_=store[:])

@@ -16,16 +16,15 @@ FP4X4 = mybir.dt.float4_e2m1fn_x4
 SIGMOID = mybir.ActivationFunctionType.Sigmoid
 COPY = mybir.ActivationFunctionType.Copy
 MULT = mybir.AluOpType.mult
-ADD = mybir.AluOpType.add
 
 P = 128
 PASSES = K // 512
 LOADS = (
     ((0, 1024, 640), (1024, 2048, 640)),
     ((0, 832, 0), (832, 1728, 576), (1728, 2048, 192)),
-    ((0, 512, 0), (512, 1024, 0), (1024, 1536, 0), (1536, 2048, 256)),
+    ((0, 512, 0), (512, 1024, 0), (1024, 1536, 0), (1536, 2048, 128)),
 )
-LAST_LOADS = ((0, 768, 0), (768, 1536, 768), (1536, 2048, 0))
+LAST_LOADS = ((0, 768), (768, 1536), (1536, 2048))
 HALF = S // 2
 SLICE = 256
 GROUP = 128
@@ -69,7 +68,7 @@ def tile_picked_idxput_gate_e_kernel(tc, xT, mem, w1_words, w1_scales, offs, slo
                 piece = keep.tile([P, 2, b - a], F32, name="raw%d_%d" % (pair, a), align_bytes=64)
                 nc.sync.dma_start(out=piece[:], in_=x_pairs[pair // 2, pair % 2, :, :, a:b])
                 raw[pair, a] = piece[:].rearrange("p e c -> p c e")
-        for a, b, split in LAST_LOADS:
+        for a, b in LAST_LOADS:
             nc.sync.dma_start(out=last_row[:, a:b], in_=x_pairs[1, 1, :, 1, a:b])
         nc.sync.dma_start(out=store[:], in_=mem)
         nc.sync.dma_start(out=w_words[:].bitcast(I32), in_=w1_words.rearrange("z p c -> p z c").bitcast(I32))
@@ -87,9 +86,7 @@ def tile_picked_idxput_gate_e_kernel(tc, xT, mem, w1_words, w1_scales, offs, slo
                 rows = raw[pair, a]
                 if split > 0:
                     nc.vector.tensor_copy(pairs[:, a : a + split, :], rows[:, 0:split, :])
-                if (pair, a) == (2, 0):
-                    nc.gpsimd.tensor_scalar(pairs[:, a:b, :], rows, 1.0, 0.0, MULT, ADD)
-                elif split < b - a:
+                if split < b - a:
                     nc.scalar.copy(pairs[:, a + split : b, :], rows[:, split : b - a, :])
             return flat[:].bitcast(U32)
 
@@ -149,23 +146,23 @@ def tile_picked_idxput_gate_e_kernel(tc, xT, mem, w1_words, w1_scales, offs, slo
             nc.vector.tensor_copy(as_words(woven1[a])[:, :, 0], window.indirect(entries(offs_sb, a, b)))
 
         last_window = keep.tile([P, T], BF16, name="last_window", tag="first_row", align_bytes=64)
-        for a, b, split in LAST_LOADS:
-            if split > 0:
-                nc.gpsimd.tensor_scalar(last_window[:, a : a + split], last_row[:, a : a + split], 1.0, 0.0, MULT, ADD)
-            if split < b - a:
-                nc.scalar.copy(last_window[:, a + split : b], last_row[:, a + split : b])
+        for a, b in LAST_LOADS:
+            nc.scalar.copy(last_window[:, a:b], last_row[:, a:b])
         for a, b in PARTS:
             nc.scalar.activation(plane(a, b, 3), last_window[:].indirect(entries(offs_sb, a, b)), COPY)
 
-        multiply(1, 0, SLICE, *quantize(1, 0, SLICE, woven1[0][:], "first"))
-        old = keep.tile([P, S], F32, name="old", tag="woven1_0", align_bytes=64)
-        nc.vector.tensor_copy(old[:], store[:].indirect(slot_sb[:]))
-        for a, b in PARTS[1:]:
+        old_rest = keep.tile([P, S - SLICE], F32, name="old_rest", align_bytes=64)
+        nc.vector.tensor_copy(old_rest[:], store[:].indirect(entries(slot_sb, SLICE, S)))
+        for a, b in PARTS[:2]:
             multiply(1, a, b, *quantize(1, a, b, woven1[a][:], "codes%d" % a))
+        old_first = keep.tile([P, SLICE], F32, name="old_first", tag="woven1_0", align_bytes=64)
+        nc.vector.tensor_copy(old_first[:], store[:].indirect(entries(slot_sb, 0, SLICE)))
+        multiply(1, HALF, S, *quantize(1, HALF, S, woven1[HALF][:], "codes%d" % HALF))
         for a, b in ((0, SLICE), (SLICE, S)):
             gate = keep.tile([P, b - a], F32, name="gate%d" % a)
             for col in range(a, b, GROUP):
                 nc.scalar.activation(gate[:, col - a : col - a + GROUP], acc[col // GROUP][:], SIGMOID)
-            nc.vector.tensor_tensor(store[:].indirect(entries(slot_sb, a, b)), old[:, a:b], gate[:], MULT)
+            old = old_first[:] if a == 0 else old_rest[:, a - SLICE : b - SLICE]
+            nc.vector.tensor_tensor(store[:].indirect(entries(slot_sb, a, b)), old, gate[:], MULT)
 
         nc.sync.dma_start(out=out, in_=store[:])

@@ -16,19 +16,22 @@ FP4X4 = mybir.dt.float4_e2m1fn_x4
 SIGMOID = mybir.ActivationFunctionType.Sigmoid
 COPY = mybir.ActivationFunctionType.Copy
 MULT = mybir.AluOpType.mult
+ADD = mybir.AluOpType.add
 
 P = 128
 PASSES = K // 512
-LOADS = (
+PAIR_LOADS = (
     ((0, 1024, 640), (1024, 2048, 640)),
     ((0, 832, 0), (832, 1728, 576), (1728, 2048, 192)),
     ((0, 512, 0), (512, 1024, 0), (1024, 1536, 0), (1536, 2048, 128)),
 )
-LAST_LOADS = ((0, 768), (768, 1536), (1536, 2048))
+LAST_LOADS = ((0, 768, 0), (768, 1536, 384), (1536, 2048, 192))
 HALF = S // 2
 SLICE = 256
 GROUP = 128
+HALVES = ((0, HALF), (HALF, S))
 PARTS = ((0, SLICE), (SLICE, HALF), (HALF, S))
+SCATTERS = ((0, SLICE), (SLICE, S))
 
 
 def tile_picked_idxput_gate_e_kernel(tc, xT, mem, w1_words, w1_scales, offs, slot, out):
@@ -49,26 +52,26 @@ def tile_picked_idxput_gate_e_kernel(tc, xT, mem, w1_words, w1_scales, offs, slo
         nc.scalar.activation(warm_out[:], warm_in[:], SIGMOID)
         nc.vector.memset(w_scales[:].bitcast(I32), 0)
 
-        x_pairs = xT.rearrange("(z p u e) t -> z u p e t", z=PASSES, u=2, e=2)
+        x_pairs = xT.rearrange("(z p u e) c -> z u p e c", z=PASSES, u=2, e=2)
         first_row = keep.tile([P, T], F32, name="first_row", align_bytes=64)
         last_row = keep.tile([P, T], F32, name="last_row", align_bytes=64)
         nc.sync.dma_start(out=first_row[:], in_=x_pairs[1, 1, :, 0, :])
         nc.sync.dma_start(offs_sb[:], offs)
-        x_flat = xT.rearrange("(z p u e) t -> z u p (e t)", z=PASSES, u=2, e=2)
+        x_runs = xT.rearrange("(z p u e) c -> z u p (e c)", z=PASSES, u=2, e=2)
         raw = {}
-        flat = keep.tile([P, 2 * T], F32, name="raw0", align_bytes=64)
+        runs = keep.tile([P, 2 * T], F32, name="raw0", align_bytes=64)
         done = 0
-        for a, b, split in LOADS[0]:
-            nc.sync.dma_start(out=flat[:, done : T + b], in_=x_flat[0, 0, :, done : T + b])
+        for a, b, split in PAIR_LOADS[0]:
+            nc.sync.dma_start(out=runs[:, done : T + b], in_=x_runs[0, 0, :, done : T + b])
             done = T + b
-            raw[0, a] = flat[:].rearrange("p (e c) -> p c e", e=2)[:, a:b, :]
+            raw[0, a] = runs[:].rearrange("p (e c) -> p c e", e=2)[:, a:b, :]
         nc.sync.dma_start(slot_sb[:], slot)
-        for pair in range(1, 3):
-            for a, b, split in LOADS[pair]:
+        for pair in range(1, len(PAIR_LOADS)):
+            for a, b, split in PAIR_LOADS[pair]:
                 piece = keep.tile([P, 2, b - a], F32, name="raw%d_%d" % (pair, a), align_bytes=64)
                 nc.sync.dma_start(out=piece[:], in_=x_pairs[pair // 2, pair % 2, :, :, a:b])
                 raw[pair, a] = piece[:].rearrange("p e c -> p c e")
-        for a, b in LAST_LOADS:
+        for a, b, split in LAST_LOADS:
             nc.sync.dma_start(out=last_row[:, a:b], in_=x_pairs[1, 1, :, 1, a:b])
         nc.sync.dma_start(out=store[:], in_=mem)
         nc.sync.dma_start(out=w_words[:].bitcast(I32), in_=w1_words.rearrange("z p c -> p z c").bitcast(I32))
@@ -78,27 +81,22 @@ def tile_picked_idxput_gate_e_kernel(tc, xT, mem, w1_words, w1_scales, offs, slo
                 in_=w1_scales[:, 4 * q : 4 * q + 4, :].rearrange("z r c -> r z c").bitcast(I32),
             )
 
-        def make_pairs(pair):
-            label = "window%d" % pair
-            flat = keep.tile([P, 2 * T], BF16, name=label, align_bytes=64)
-            pairs = flat[:].rearrange("p (t e) -> p t e", e=2)
-            for a, b, split in LOADS[pair]:
+        def round_pair(pair):
+            rounded = keep.tile([P, 2 * T], BF16, name="window%d" % pair, align_bytes=64)
+            side_by_side = rounded[:].rearrange("p (c e) -> p c e", e=2)
+            for a, b, split in PAIR_LOADS[pair]:
                 rows = raw[pair, a]
                 if split > 0:
-                    nc.vector.tensor_copy(pairs[:, a : a + split, :], rows[:, 0:split, :])
-                if split < b - a:
-                    nc.scalar.copy(pairs[:, a + split : b, :], rows[:, split : b - a, :])
-            return flat[:].bitcast(U32)
+                    nc.vector.tensor_copy(side_by_side[:, a : a + split, :], rows[:, 0:split, :])
+                nc.scalar.copy(side_by_side[:, a + split : b, :], rows[:, split : b - a, :])
+            return rounded[:].bitcast(U32)
 
         acc = [psum.tile([P, GROUP], F32, name="acc%d" % g) for g in range(S // GROUP)]
 
-        def quantize(z, a, b, woven, tag):
+        def quantize_and_multiply(z, a, b, woven, tag):
             codes = keep.tile([P, b - a], U32, name="codes%d_%d" % (z, a), tag=tag, align_bytes=64)
             scales = keep.tile([P, b - a], U8, name="scales%d_%d" % (z, a), align_bytes=64)
-            nc.vector.quantize_mx(out=codes[:].bitcast(FP8X4), scales=scales[:], in_=woven)
-            return codes, scales
-
-        def multiply(z, a, b, codes, scales):
+            nc.vector.quantize_mx(out=codes[:].bitcast(FP8X4), scales=scales[:], in_=woven[:])
             for col in range(0, b - a, GROUP):
                 nc.tensor.matmul_mx(
                     out=acc[(a + col) // GROUP][:],
@@ -113,56 +111,51 @@ def tile_picked_idxput_gate_e_kernel(tc, xT, mem, w1_words, w1_scales, offs, slo
         def entries(index_tile, a, b):
             return index_tile[:, a // 16 : b // 16]
 
-        def as_words(woven):
-            return woven[:].bitcast(U32).rearrange("p (n u) -> p n u", u=2)
-
-        picked0 = [keep.tile([P, 2, HALF], U32, name="picked0_%d" % h, align_bytes=64) for h in range(2)]
-        woven0 = [keep.tile([P, 4 * HALF], BF16, name="woven0_%d" % h, align_bytes=64) for h in range(2)]
+        picked0 = {a: keep.tile([P, 2, b - a], U32, name="picked0_%d" % a, align_bytes=64) for a, b in HALVES}
+        woven0 = {a: keep.tile([P, 4 * (b - a)], BF16, name="woven0_%d" % a, align_bytes=64) for a, b in HALVES}
         woven1 = {a: keep.tile([P, 4 * (b - a)], BF16, name="woven1_%d" % a, align_bytes=64) for a, b in PARTS}
 
-        def woven1_cols(a, b):
-            first = max(start for start in woven1 if start <= a)
-            return woven1[first][:, 4 * (a - first) : 4 * (b - first)]
-
-        def plane(a, b, t):
-            return woven1_cols(a, b).rearrange("p (n t) -> p n t", t=4)[:, :, t]
+        def row_places(a, t):
+            return woven1[a][:].rearrange("p (n t) -> p n t", t=4)[:, :, t]
 
         for a, b in PARTS:
-            nc.vector.tensor_copy(plane(a, b, 2), first_row[:].indirect(entries(offs_sb, a, b)))
+            nc.vector.tensor_copy(row_places(a, 2), first_row[:].indirect(entries(offs_sb, a, b)))
+
         for u in range(2):
-            window = make_pairs(u)
-            for h in range(2):
-                nc.vector.tensor_copy(picked0[h][:, u, :], window.indirect(entries(offs_sb, h * HALF, (h + 1) * HALF)))
-        for h in range(2):
+            window = round_pair(u)
+            for a, b in HALVES:
+                nc.vector.tensor_copy(picked0[a][:, u, :], window.indirect(entries(offs_sb, a, b)))
+        for a, b in HALVES:
             nc.vector.tensor_copy(
-                woven0[h][:].bitcast(I32).rearrange("p (n u) -> p n u", u=2),
-                picked0[h][:].bitcast(I32).rearrange("p u n -> p n u"),
+                woven0[a][:].bitcast(I32).rearrange("p (n u) -> p n u", u=2),
+                picked0[a][:].bitcast(I32).rearrange("p u n -> p n u"),
             )
+        for a, b in HALVES:
+            quantize_and_multiply(0, a, b, woven0[a], "codes_half%d" % (a // HALF))
+
+        window = round_pair(2)
         for a, b in PARTS:
-            woven = woven0[a // HALF][:, 4 * (a % HALF) : 4 * (a % HALF + b - a)]
-            multiply(0, a, b, *quantize(0, a, b, woven, "codes%d" % a))
-        window = make_pairs(2)
-        for a, b in PARTS:
-            nc.vector.tensor_copy(as_words(woven1[a])[:, :, 0], window.indirect(entries(offs_sb, a, b)))
+            words = woven1[a][:].bitcast(U32).rearrange("p (n u) -> p n u", u=2)
+            nc.vector.tensor_copy(words[:, :, 0], window.indirect(entries(offs_sb, a, b)))
 
         last_window = keep.tile([P, T], BF16, name="last_window", tag="first_row", align_bytes=64)
-        for a, b in LAST_LOADS:
-            nc.scalar.copy(last_window[:, a:b], last_row[:, a:b])
+        for a, b, split in LAST_LOADS:
+            if split > 0:
+                nc.gpsimd.tensor_scalar(last_window[:, a : a + split], last_row[:, a : a + split], 1.0, 0.0, MULT, ADD)
+            nc.scalar.copy(last_window[:, a + split : b], last_row[:, a + split : b])
         for a, b in PARTS:
-            nc.scalar.activation(plane(a, b, 3), last_window[:].indirect(entries(offs_sb, a, b)), COPY)
+            nc.scalar.activation(row_places(a, 3), last_window[:].indirect(entries(offs_sb, a, b)), COPY)
 
-        old_rest = keep.tile([P, S - SLICE], F32, name="old_rest", align_bytes=64)
-        nc.vector.tensor_copy(old_rest[:], store[:].indirect(entries(slot_sb, SLICE, S)))
-        for a, b in PARTS[:2]:
-            multiply(1, a, b, *quantize(1, a, b, woven1[a][:], "codes%d" % a))
-        old_first = keep.tile([P, SLICE], F32, name="old_first", tag="woven1_0", align_bytes=64)
-        nc.vector.tensor_copy(old_first[:], store[:].indirect(entries(slot_sb, 0, SLICE)))
-        multiply(1, HALF, S, *quantize(1, HALF, S, woven1[HALF][:], "codes%d" % HALF))
-        for a, b in ((0, SLICE), (SLICE, S)):
+        quantize_and_multiply(1, 0, SLICE, woven1[0], "codes_first")
+        old = keep.tile([P, S], F32, name="old", align_bytes=64)
+        nc.vector.tensor_copy(old[:], store[:].indirect(slot_sb[:]))
+        for a, b in PARTS[1:]:
+            quantize_and_multiply(1, a, b, woven1[a], "codes_half%d" % (a // HALF))
+
+        for a, b in SCATTERS:
             gate = keep.tile([P, b - a], F32, name="gate%d" % a)
             for col in range(a, b, GROUP):
                 nc.scalar.activation(gate[:, col - a : col - a + GROUP], acc[col // GROUP][:], SIGMOID)
-            old = old_first[:] if a == 0 else old_rest[:, a - SLICE : b - SLICE]
-            nc.vector.tensor_tensor(store[:].indirect(entries(slot_sb, a, b)), old, gate[:], MULT)
+            nc.vector.tensor_tensor(store[:].indirect(entries(slot_sb, a, b)), old[:, a:b], gate[:], MULT)
 
         nc.sync.dma_start(out=out, in_=store[:])

@@ -20,18 +20,11 @@ ADD = mybir.AluOpType.add
 
 P = 128
 PASSES = K // 512
-PAIR_LOADS = (
-    ((0, 1024, 640), (1024, 2048, 640)),
-    ((0, 832, 0), (832, 1728, 576), (1728, 2048, 192)),
-    ((0, 512, 0), (512, 1024, 0), (1024, 1536, 0), (1536, 2048, 128)),
-)
-LAST_LOADS = ((0, 768, 0), (768, 1536, 384), (1536, 2048, 192))
-HALF = S // 2
+
 SLICE = 256
-GROUP = 128
-HALVES = ((0, HALF), (HALF, S))
-PARTS = ((0, SLICE), (SLICE, HALF), (HALF, S))
-SCATTERS = ((0, SLICE), (SLICE, S))
+SLICES = S // SLICE
+SCALAR_PUTS = 512
+MERGES = ((0, 256), (256, 768), (768, 1280), (1280, 1792), (1792, 2048))
 
 
 def tile_picked_idxput_gate_e_kernel(tc, xT, mem, w1_words, w1_scales, offs, slot, out):
@@ -41,6 +34,7 @@ def tile_picked_idxput_gate_e_kernel(tc, xT, mem, w1_words, w1_scales, offs, slo
         psum = ctx.enter_context(tc.psum_pool(name="psum", bufs=1))
 
         store = keep.tile([P, U], F32, name="store")
+        side = keep.tile([P, U], F32, name="side")
         slot_sb = keep.tile([P, S // 16], U16, name="slot_sb")
         offs_sb = keep.tile([P, S // 16], U16, name="offs_sb")
         w_words = keep.tile([P, PASSES, 2 * N], U8, name="w_words", align_bytes=64)
@@ -51,29 +45,17 @@ def tile_picked_idxput_gate_e_kernel(tc, xT, mem, w1_words, w1_scales, offs, slo
         nc.vector.memset(warm_in[:], 0.0)
         nc.scalar.activation(warm_out[:], warm_in[:], SIGMOID)
         nc.vector.memset(w_scales[:].bitcast(I32), 0)
+        nc.vector.memset(side[:], 0.0)
 
-        x_pairs = xT.rearrange("(z p u e) c -> z u p e c", z=PASSES, u=2, e=2)
-        first_row = keep.tile([P, T], F32, name="first_row", align_bytes=64)
-        last_row = keep.tile([P, T], F32, name="last_row", align_bytes=64)
-        nc.sync.dma_start(out=first_row[:], in_=x_pairs[1, 1, :, 0, :])
-        nc.sync.dma_start(offs_sb[:], offs)
-        x_runs = xT.rearrange("(z p u e) c -> z u p (e c)", z=PASSES, u=2, e=2)
-        raw = {}
-        runs = keep.tile([P, 2 * T], F32, name="raw0", align_bytes=64)
-        done = 0
-        for a, b, split in PAIR_LOADS[0]:
-            nc.sync.dma_start(out=runs[:, done : T + b], in_=x_runs[0, 0, :, done : T + b])
-            done = T + b
-            raw[0, a] = runs[:].rearrange("p (e c) -> p c e", e=2)[:, a:b, :]
-        nc.sync.dma_start(slot_sb[:], slot)
-        for pair in range(1, len(PAIR_LOADS)):
-            for a, b, split in PAIR_LOADS[pair]:
-                piece = keep.tile([P, 2, b - a], F32, name="raw%d_%d" % (pair, a), align_bytes=64)
-                nc.sync.dma_start(out=piece[:], in_=x_pairs[pair // 2, pair % 2, :, :, a:b])
-                raw[pair, a] = piece[:].rearrange("p e c -> p c e")
-        for a, b, split in LAST_LOADS:
-            nc.sync.dma_start(out=last_row[:, a:b], in_=x_pairs[1, 1, :, 1, a:b])
+        x_rows = xT.rearrange("(z p t) c -> z t p c", z=PASSES, t=4)
         nc.sync.dma_start(out=store[:], in_=mem)
+        nc.sync.dma_start(slot_sb[:], slot)
+        nc.sync.dma_start(offs_sb[:], offs)
+        rows = {}
+        for z in range(PASSES):
+            for t in range(4):
+                rows[z, t] = keep.tile([P, T], F32, name="row%d_%d" % (z, t), align_bytes=64)
+                nc.sync.dma_start(out=rows[z, t][:], in_=x_rows[z, t])
         nc.sync.dma_start(out=w_words[:].bitcast(I32), in_=w1_words.rearrange("z p c -> p z c").bitcast(I32))
         for q in range(4):
             nc.sync.dma_start(
@@ -81,81 +63,77 @@ def tile_picked_idxput_gate_e_kernel(tc, xT, mem, w1_words, w1_scales, offs, slo
                 in_=w1_scales[:, 4 * q : 4 * q + 4, :].rearrange("z r c -> r z c").bitcast(I32),
             )
 
-        def round_pair(pair):
-            rounded = keep.tile([P, 2 * T], BF16, name="window%d" % pair, align_bytes=64)
-            side_by_side = rounded[:].rearrange("p (c e) -> p c e", e=2)
-            for a, b, split in PAIR_LOADS[pair]:
-                rows = raw[pair, a]
-                if split > 0:
-                    nc.vector.tensor_copy(side_by_side[:, a : a + split, :], rows[:, 0:split, :])
-                nc.scalar.copy(side_by_side[:, a + split : b, :], rows[:, split : b - a, :])
-            return rounded[:].bitcast(U32)
-
-        acc = [psum.tile([P, GROUP], F32, name="acc%d" % g) for g in range(S // GROUP)]
-
-        def quantize_and_multiply(z, a, b, woven, tag):
-            codes = keep.tile([P, b - a], U32, name="codes%d_%d" % (z, a), tag=tag, align_bytes=64)
-            scales = keep.tile([P, b - a], U8, name="scales%d_%d" % (z, a), align_bytes=64)
-            nc.vector.quantize_mx(out=codes[:].bitcast(FP8X4), scales=scales[:], in_=woven[:])
-            for col in range(0, b - a, GROUP):
-                nc.tensor.matmul_mx(
-                    out=acc[(a + col) // GROUP][:],
-                    lhsT=w_words[:, z, :].bitcast(FP4X4),
-                    lhsT_scale=w_scales[:, z, :],
-                    rhs=codes[:, col : col + GROUP].bitcast(FP8X4),
-                    rhs_scale=scales[:, col : col + GROUP],
-                    start=(z == 0),
-                    stop=(z == PASSES - 1),
-                )
-
         def entries(index_tile, a, b):
             return index_tile[:, a // 16 : b // 16]
 
-        picked0 = {a: keep.tile([P, 2, b - a], U32, name="picked0_%d" % a, align_bytes=64) for a, b in HALVES}
-        woven0 = {a: keep.tile([P, 4 * (b - a)], BF16, name="woven0_%d" % a, align_bytes=64) for a, b in HALVES}
-        woven1 = {a: keep.tile([P, 4 * (b - a)], BF16, name="woven1_%d" % a, align_bytes=64) for a, b in PARTS}
-
-        def row_places(a, t):
-            return woven1[a][:].rearrange("p (n t) -> p n t", t=4)[:, :, t]
-
-        for a, b in PARTS:
-            nc.vector.tensor_copy(row_places(a, 2), first_row[:].indirect(entries(offs_sb, a, b)))
-
-        for u in range(2):
-            window = round_pair(u)
-            for a, b in HALVES:
-                nc.vector.tensor_copy(picked0[a][:, u, :], window.indirect(entries(offs_sb, a, b)))
-        for a, b in HALVES:
-            nc.vector.tensor_copy(
-                woven0[a][:].bitcast(I32).rearrange("p (n u) -> p n u", u=2),
-                picked0[a][:].bitcast(I32).rearrange("p u n -> p n u"),
-            )
-        for a, b in HALVES:
-            quantize_and_multiply(0, a, b, woven0[a], "codes_half%d" % (a // HALF))
-
-        window = round_pair(2)
-        for a, b in PARTS:
-            words = woven1[a][:].bitcast(U32).rearrange("p (n u) -> p n u", u=2)
-            nc.vector.tensor_copy(words[:, :, 0], window.indirect(entries(offs_sb, a, b)))
-
-        last_window = keep.tile([P, T], BF16, name="last_window", tag="first_row", align_bytes=64)
-        for a, b, split in LAST_LOADS:
-            if split > 0:
-                nc.gpsimd.tensor_scalar(last_window[:, a : a + split], last_row[:, a : a + split], 1.0, 0.0, MULT, ADD)
-            nc.scalar.copy(last_window[:, a + split : b], last_row[:, a + split : b])
-        for a, b in PARTS:
-            nc.scalar.activation(row_places(a, 3), last_window[:].indirect(entries(offs_sb, a, b)), COPY)
-
-        quantize_and_multiply(1, 0, SLICE, woven1[0], "codes_first")
         old = keep.tile([P, S], F32, name="old", align_bytes=64)
-        nc.vector.tensor_copy(old[:], store[:].indirect(slot_sb[:]))
-        for a, b in PARTS[1:]:
-            quantize_and_multiply(1, a, b, woven1[a], "codes_half%d" % (a // HALF))
+        nc.scalar.activation(old[:, 0:512], store[:].indirect(entries(slot_sb, 0, 512)), COPY)
+        nc.vector.tensor_copy(old[:, 512:S], store[:].indirect(entries(slot_sb, 512, S)))
+        nc.vector.tensor_copy(store[:].indirect(entries(slot_sb, 0, SCALAR_PUTS)), side[:, 0:SCALAR_PUTS])
 
-        for a, b in SCATTERS:
-            gate = keep.tile([P, b - a], F32, name="gate%d" % a)
-            for col in range(a, b, GROUP):
-                nc.scalar.activation(gate[:, col - a : col - a + GROUP], acc[col // GROUP][:], SIGMOID)
-            nc.vector.tensor_tensor(store[:].indirect(entries(slot_sb, a, b)), old[:, a:b], gate[:], MULT)
+        acc = [psum.tile([P, SLICE], F32, name="acc%d" % g) for g in range(SLICES)]
+        woven = {}
+        planes = {}
+        for z in range(PASSES):
+            for s in range(SLICES):
+                woven[z, s] = keep.tile([P, SLICE, 4], BF16, name="woven%d_%d" % (z, s), align_bytes=64)
+            for u in range(2):
+                planes[z, u] = keep.tile([P, 2, S - SLICE], BF16, name="planes%d_%d" % (z, u), align_bytes=64)
 
-        nc.sync.dma_start(out=out, in_=store[:])
+        def gather(z, t):
+            nc.vector.tensor_copy(woven[z, 0][:, :, t], rows[z, t][:].indirect(entries(offs_sb, 0, SLICE)))
+            width = SLICE if (z, t) == (PASSES - 1, 3) else S - SLICE
+            for a in range(SLICE, S, width):
+                nc.scalar.activation(
+                    planes[z, t // 2][:, t % 2, a - SLICE : a - SLICE + width],
+                    rows[z, t][:].indirect(entries(offs_sb, a, a + width)),
+                    COPY,
+                )
+
+        def place(z, s, u):
+            nc.vector.tensor_copy(
+                woven[z, s][:, :, 2 * u : 2 * u + 2], planes[z, u][:, :, (s - 1) * SLICE : s * SLICE].rearrange("p e n -> p n e")
+            )
+
+        def multiply(z, s):
+            codes = keep.tile([P, SLICE], U32, name="codes%d_%d" % (z, s), align_bytes=64)
+            scales = keep.tile([P, SLICE], U8, name="scales%d_%d" % (z, s), align_bytes=64)
+            nc.vector.quantize_mx(
+                out=codes[:].bitcast(FP8X4), scales=scales[:], in_=woven[z, s][:].rearrange("p n t -> p (n t)")
+            )
+            nc.tensor.matmul_mx(
+                out=acc[s][:],
+                lhsT=w_words[:, z, :].bitcast(FP4X4),
+                lhsT_scale=w_scales[:, z, :],
+                rhs=codes[:].bitcast(FP8X4),
+                rhs_scale=scales[:],
+                start=(z == 0),
+                stop=(z == PASSES - 1),
+            )
+
+        for z in range(PASSES):
+            gather(z, 0)
+            gather(z, 1)
+            for s in range(1, SLICES):
+                place(z, s, 0)
+            gather(z, 2)
+            gather(z, 3)
+            for s in range(SLICES):
+                if s + 1 < SLICES:
+                    place(z, s + 1, 1)
+                multiply(z, s)
+
+        gate = [keep.tile([P, S // 2], F32, name="gate%d" % h) for h in range(2)]
+        for s in range(SLICES):
+            nc.scalar.activation(gate[s // 2][:, (s % 2) * SLICE : (s % 2 + 1) * SLICE], acc[s][:], SIGMOID)
+        fresh = keep.tile([P, SCALAR_PUTS], F32, name="fresh")
+        for a in range(0, SCALAR_PUTS, SLICE):
+            nc.vector.tensor_tensor(fresh[:, a : a + SLICE], old[:, a : a + SLICE], gate[0][:, a : a + SLICE], MULT)
+        for a in range(0, SCALAR_PUTS, SLICE):
+            nc.scalar.activation(side[:].indirect(entries(slot_sb, a, a + SLICE)), fresh[:, a : a + SLICE], COPY)
+        nc.vector.tensor_tensor(store[:].indirect(entries(slot_sb, SCALAR_PUTS, S)), old[:, SCALAR_PUTS:S], gate[1][:], MULT)
+
+        for a, b in MERGES:
+            merged = keep.tile([P, b - a], F32, name="merged%d" % a)
+            nc.vector.tensor_tensor(merged[:], store[:, a:b], side[:, a:b], ADD)
+            nc.sync.dma_start(out=out[:, a:b], in_=merged[:])

@@ -23,7 +23,7 @@ PASSES = K // 512
 
 SLICE = 256
 SLICES = S // SLICE
-SCALAR_PUTS = 512
+SCALAR_SLICES = (0, 2)
 MERGES = ((0, 256), (256, 768), (768, 1280), (1280, 1792), (1792, 2048))
 
 
@@ -51,17 +51,17 @@ def tile_picked_idxput_gate_e_kernel(tc, xT, mem, w1_words, w1_scales, offs, slo
         nc.sync.dma_start(out=store[:], in_=mem)
         nc.sync.dma_start(slot_sb[:], slot)
         nc.sync.dma_start(offs_sb[:], offs)
+        for q in range(4):
+            nc.sync.dma_start(
+                out=w_scales[32 * q : 32 * q + 4, :, :].bitcast(I32),
+                in_=w1_scales[:, 4 * q : 4 * q + 4, :].rearrange("z r c -> r z c").bitcast(I32),
+            )
         rows = {}
         for z in range(PASSES):
             for t in range(4):
                 rows[z, t] = keep.tile([P, T], F32, name="row%d_%d" % (z, t), align_bytes=64)
                 nc.sync.dma_start(out=rows[z, t][:], in_=x_rows[z, t])
         nc.sync.dma_start(out=w_words[:].bitcast(I32), in_=w1_words.rearrange("z p c -> p z c").bitcast(I32))
-        for q in range(4):
-            nc.sync.dma_start(
-                out=w_scales[32 * q : 32 * q + 4, :, :].bitcast(I32),
-                in_=w1_scales[:, 4 * q : 4 * q + 4, :].rearrange("z r c -> r z c").bitcast(I32),
-            )
 
         def entries(index_tile, a, b):
             return index_tile[:, a // 16 : b // 16]
@@ -69,9 +69,10 @@ def tile_picked_idxput_gate_e_kernel(tc, xT, mem, w1_words, w1_scales, offs, slo
         old = keep.tile([P, S], F32, name="old", align_bytes=64)
         nc.scalar.activation(old[:, 0:512], store[:].indirect(entries(slot_sb, 0, 512)), COPY)
         nc.vector.tensor_copy(old[:, 512:S], store[:].indirect(entries(slot_sb, 512, S)))
-        nc.vector.tensor_copy(store[:].indirect(entries(slot_sb, 0, SCALAR_PUTS)), side[:, 0:SCALAR_PUTS])
+        for s in SCALAR_SLICES:
+            nc.vector.tensor_copy(store[:].indirect(entries(slot_sb, s * SLICE, (s + 1) * SLICE)), side[:, 0:SLICE])
 
-        acc = [psum.tile([P, SLICE], F32, name="acc%d" % g) for g in range(SLICES)]
+        acc = {}
         woven = {}
         planes = {}
         for z in range(PASSES):
@@ -95,21 +96,46 @@ def tile_picked_idxput_gate_e_kernel(tc, xT, mem, w1_words, w1_scales, offs, slo
                 woven[z, s][:, :, 2 * u : 2 * u + 2], planes[z, u][:, :, (s - 1) * SLICE : s * SLICE].rearrange("p e n -> p n e")
             )
 
-        def multiply(z, s):
-            codes = keep.tile([P, SLICE], U32, name="codes%d_%d" % (z, s), align_bytes=64)
-            scales = keep.tile([P, SLICE], U8, name="scales%d_%d" % (z, s), align_bytes=64)
+        codes = {}
+        scales = {}
+
+        def quantise(z, s):
+            codes[z, s] = keep.tile([P, SLICE], U32, name="codes%d_%d" % (z, s), align_bytes=64)
+            scales[z, s] = keep.tile([P, SLICE], U8, name="scales%d_%d" % (z, s), align_bytes=64)
             nc.vector.quantize_mx(
-                out=codes[:].bitcast(FP8X4), scales=scales[:], in_=woven[z, s][:].rearrange("p n t -> p (n t)")
+                out=codes[z, s][:].bitcast(FP8X4), scales=scales[z, s][:], in_=woven[z, s][:].rearrange("p n t -> p (n t)")
             )
-            nc.tensor.matmul_mx(
-                out=acc[s][:],
-                lhsT=w_words[:, z, :].bitcast(FP4X4),
-                lhsT_scale=w_scales[:, z, :],
-                rhs=codes[:].bitcast(FP8X4),
-                rhs_scale=scales[:],
-                start=(z == 0),
-                stop=(z == PASSES - 1),
-            )
+
+        def multiply(s):
+            acc[s] = psum.tile([P, SLICE], F32, name="acc%d" % s, tag="bank%d" % min(s, SLICES - 2))
+            for z in range(PASSES):
+                nc.tensor.matmul_mx(
+                    out=acc[s][:],
+                    lhsT=w_words[:, z, :].bitcast(FP4X4),
+                    lhsT_scale=w_scales[:, z, :],
+                    rhs=codes[z, s][:].bitcast(FP8X4),
+                    rhs_scale=scales[z, s][:],
+                    start=(z == 0),
+                    stop=(z == PASSES - 1),
+                )
+
+        gate = [keep.tile([P, SLICE], F32, name="gate%d" % s) for s in range(SLICES)]
+        fresh = {}
+
+        def squash(s):
+            multiply(s)
+            nc.scalar.activation(gate[s][:], acc[s][:], SIGMOID)
+
+        def renew(s):
+            fresh[s] = keep.tile([P, SLICE], F32, name="fresh%d" % s)
+            nc.vector.tensor_tensor(fresh[s][:], old[:, s * SLICE : (s + 1) * SLICE], gate[s][:], MULT)
+
+        def put(s):
+            a, b = s * SLICE, (s + 1) * SLICE
+            if s in SCALAR_SLICES:
+                nc.scalar.activation(side[:].indirect(entries(slot_sb, a, b)), fresh[s][:], COPY)
+            else:
+                nc.vector.tensor_tensor(store[:].indirect(entries(slot_sb, a, b)), old[:, a:b], gate[s][:], MULT)
 
         for z in range(PASSES):
             gather(z, 0)
@@ -118,20 +144,28 @@ def tile_picked_idxput_gate_e_kernel(tc, xT, mem, w1_words, w1_scales, offs, slo
                 place(z, s, 0)
             gather(z, 2)
             gather(z, 3)
-            for s in range(SLICES):
-                if s + 1 < SLICES:
-                    place(z, s + 1, 1)
-                multiply(z, s)
+            if z == 0:
+                for s in range(SLICES):
+                    if s + 1 < SLICES:
+                        place(z, s + 1, 1)
+                    quantise(z, s)
 
-        gate = [keep.tile([P, S // 2], F32, name="gate%d" % h) for h in range(2)]
-        for s in range(SLICES):
-            nc.scalar.activation(gate[s // 2][:, (s % 2) * SLICE : (s % 2 + 1) * SLICE], acc[s][:], SIGMOID)
-        fresh = keep.tile([P, SCALAR_PUTS], F32, name="fresh")
-        for a in range(0, SCALAR_PUTS, SLICE):
-            nc.vector.tensor_tensor(fresh[:, a : a + SLICE], old[:, a : a + SLICE], gate[0][:, a : a + SLICE], MULT)
-        for a in range(0, SCALAR_PUTS, SLICE):
-            nc.scalar.activation(side[:].indirect(entries(slot_sb, a, a + SLICE)), fresh[:, a : a + SLICE], COPY)
-        nc.vector.tensor_tensor(store[:].indirect(entries(slot_sb, SCALAR_PUTS, S)), old[:, SCALAR_PUTS:S], gate[1][:], MULT)
+        place(1, 1, 1)
+        quantise(1, 0)
+        place(1, 2, 1)
+        quantise(1, 1)
+        quantise(1, 2)
+        place(1, 3, 1)
+        for s in range(SLICES - 1):
+            squash(s)
+        renew(0)
+        quantise(1, 3)
+        put(0)
+        squash(3)
+        put(1)
+        renew(2)
+        put(2)
+        put(3)
 
         for a, b in MERGES:
             merged = keep.tile([P, b - a], F32, name="merged%d" % a)

@@ -24,7 +24,7 @@ PASSES = K // 512
 SLICE = 256
 SLICES = S // SLICE
 SCALAR_SLICES = (0, 2)
-MERGES = ((0, 256), (256, 768), (768, 1280), (1280, 1792), (1792, 2048))
+MERGES = ((0, 256), (256, 640), (640, 1088), (1088, 1568), (1568, 2048))
 
 
 def tile_picked_idxput_gate_e_kernel(tc, xT, mem, w1_words, w1_scales, offs, slot, out):

@@ -23,7 +23,8 @@ PASSES = K // 512
 
 SLICE = 256
 SLICES = S // SLICE
-SCALAR_SLICES = (0, 2)
+SCALAR_PUTS = 2 * SLICE
+ORDER = (0, 2, 1, 3)
 MERGES = ((0, 256), (256, 640), (640, 1088), (1088, 1568), (1568, 2048))
 
 
@@ -69,103 +70,93 @@ def tile_picked_idxput_gate_e_kernel(tc, xT, mem, w1_words, w1_scales, offs, slo
         old = keep.tile([P, S], F32, name="old", align_bytes=64)
         nc.scalar.activation(old[:, 0:512], store[:].indirect(entries(slot_sb, 0, 512)), COPY)
         nc.vector.tensor_copy(old[:, 512:S], store[:].indirect(entries(slot_sb, 512, S)))
-        for s in SCALAR_SLICES:
-            nc.vector.tensor_copy(store[:].indirect(entries(slot_sb, s * SLICE, (s + 1) * SLICE)), side[:, 0:SLICE])
+        nc.vector.tensor_copy(store[:].indirect(entries(slot_sb, 0, SCALAR_PUTS)), side[:, 0:SCALAR_PUTS])
 
-        acc = {}
-        woven = {}
+        woven = [keep.tile([P, S, 4], BF16, name="woven%d" % z, align_bytes=64) for z in range(PASSES)]
+        codes = [keep.tile([P, S], U32, name="codes%d" % z, align_bytes=64) for z in range(PASSES)]
+        scales = [keep.tile([P, S], U8, name="scales%d" % z, align_bytes=64) for z in range(PASSES)]
         planes = {}
         for z in range(PASSES):
-            for s in range(SLICES):
-                woven[z, s] = keep.tile([P, SLICE, 4], BF16, name="woven%d_%d" % (z, s), align_bytes=64)
             for u in range(2):
                 planes[z, u] = keep.tile([P, 2, S - SLICE], BF16, name="planes%d_%d" % (z, u), align_bytes=64)
 
-        def gather(z, t):
-            nc.vector.tensor_copy(woven[z, 0][:, :, t], rows[z, t][:].indirect(entries(offs_sb, 0, SLICE)))
-            width = SLICE if (z, t) == (PASSES - 1, 3) else S - SLICE
-            for a in range(SLICE, S, width):
+        def span(s):
+            return s * SLICE, (s + 1) * SLICE
+
+        def gather(z, t, spans):
+            nc.vector.tensor_copy(woven[z][:, 0:SLICE, t], rows[z, t][:].indirect(entries(offs_sb, 0, SLICE)))
+            for a, b in spans:
                 nc.scalar.activation(
-                    planes[z, t // 2][:, t % 2, a - SLICE : a - SLICE + width],
-                    rows[z, t][:].indirect(entries(offs_sb, a, a + width)),
-                    COPY,
+                    planes[z, t // 2][:, t % 2, a - SLICE : b - SLICE], rows[z, t][:].indirect(entries(offs_sb, a, b)), COPY
                 )
 
-        def place(z, s, u):
+        def place(z, u, a, b):
             nc.vector.tensor_copy(
-                woven[z, s][:, :, 2 * u : 2 * u + 2], planes[z, u][:, :, (s - 1) * SLICE : s * SLICE].rearrange("p e n -> p n e")
+                woven[z][:, a:b, 2 * u : 2 * u + 2], planes[z, u][:, :, a - SLICE : b - SLICE].rearrange("p e n -> p n e")
             )
 
-        codes = {}
-        scales = {}
-
-        def quantise(z, s):
-            codes[z, s] = keep.tile([P, SLICE], U32, name="codes%d_%d" % (z, s), align_bytes=64)
-            scales[z, s] = keep.tile([P, SLICE], U8, name="scales%d_%d" % (z, s), align_bytes=64)
+        def quantise(z, a, b):
             nc.vector.quantize_mx(
-                out=codes[z, s][:].bitcast(FP8X4), scales=scales[z, s][:], in_=woven[z, s][:].rearrange("p n t -> p (n t)")
+                out=codes[z][:, a:b].bitcast(FP8X4), scales=scales[z][:, a:b], in_=woven[z][:, a:b, :].rearrange("p n t -> p (n t)")
             )
-
-        def multiply(s):
-            acc[s] = psum.tile([P, SLICE], F32, name="acc%d" % s, tag="bank%d" % min(s, SLICES - 2))
-            for z in range(PASSES):
-                nc.tensor.matmul_mx(
-                    out=acc[s][:],
-                    lhsT=w_words[:, z, :].bitcast(FP4X4),
-                    lhsT_scale=w_scales[:, z, :],
-                    rhs=codes[z, s][:].bitcast(FP8X4),
-                    rhs_scale=scales[z, s][:],
-                    start=(z == 0),
-                    stop=(z == PASSES - 1),
-                )
 
         gate = [keep.tile([P, SLICE], F32, name="gate%d" % s) for s in range(SLICES)]
         fresh = {}
 
-        def squash(s):
-            multiply(s)
-            nc.scalar.activation(gate[s][:], acc[s][:], SIGMOID)
+        def squash(s, bank):
+            a, b = span(s)
+            acc = psum.tile([P, SLICE], F32, name="acc%d" % s, tag="bank%d" % bank)
+            for z in range(PASSES):
+                nc.tensor.matmul_mx(
+                    out=acc[:],
+                    lhsT=w_words[:, z, :].bitcast(FP4X4),
+                    lhsT_scale=w_scales[:, z, :],
+                    rhs=codes[z][:, a:b].bitcast(FP8X4),
+                    rhs_scale=scales[z][:, a:b],
+                    start=(z == 0),
+                    stop=(z == PASSES - 1),
+                )
+            nc.scalar.activation(gate[s][:], acc[:], SIGMOID)
 
         def renew(s):
+            a, b = span(s)
             fresh[s] = keep.tile([P, SLICE], F32, name="fresh%d" % s)
-            nc.vector.tensor_tensor(fresh[s][:], old[:, s * SLICE : (s + 1) * SLICE], gate[s][:], MULT)
+            nc.vector.tensor_tensor(fresh[s][:], old[:, a:b], gate[s][:], MULT)
 
         def put(s):
-            a, b = s * SLICE, (s + 1) * SLICE
-            if s in SCALAR_SLICES:
+            a, b = span(s)
+            if a < SCALAR_PUTS:
                 nc.scalar.activation(side[:].indirect(entries(slot_sb, a, b)), fresh[s][:], COPY)
             else:
                 nc.vector.tensor_tensor(store[:].indirect(entries(slot_sb, a, b)), old[:, a:b], gate[s][:], MULT)
 
-        for z in range(PASSES):
-            gather(z, 0)
-            gather(z, 1)
-            for s in range(1, SLICES):
-                place(z, s, 0)
-            gather(z, 2)
-            gather(z, 3)
-            if z == 0:
-                for s in range(SLICES):
-                    if s + 1 < SLICES:
-                        place(z, s + 1, 1)
-                    quantise(z, s)
+        rest = (SLICE, S)
+        for z, u in ((0, 0), (0, 1), (1, 0)):
+            gather(z, 2 * u, [rest])
+            gather(z, 2 * u + 1, [rest])
+            place(z, u, *rest)
+            if u == 1:
+                quantise(z, 0, S)
+        gather(1, 2, [rest])
 
-        place(1, 1, 1)
-        quantise(1, 0)
-        place(1, 2, 1)
-        quantise(1, 1)
-        quantise(1, 2)
-        place(1, 3, 1)
-        for s in range(SLICES - 1):
-            squash(s)
-        renew(0)
-        quantise(1, 3)
-        put(0)
-        squash(3)
-        put(1)
-        renew(2)
-        put(2)
-        put(3)
+        first, second, third, last = ORDER
+        gather(1, 3, [span(s) for s in (second, third, last)])
+        place(1, 1, *span(second))
+        quantise(1, *span(first))
+        place(1, 1, *span(third))
+        quantise(1, *span(second))
+        quantise(1, *span(third))
+        place(1, 1, *span(last))
+        for bank, s in enumerate((first, second, third)):
+            squash(s, bank)
+        renew(first)
+        quantise(1, *span(last))
+        put(first)
+        squash(last, 2)
+        put(second)
+        renew(third)
+        put(third)
+        put(last)
 
         for a, b in MERGES:
             merged = keep.tile([P, b - a], F32, name="merged%d" % a)

@@ -23,8 +23,9 @@ PASSES = K // 512
 
 SLICE = 256
 SLICES = S // SLICE
-SCALAR_PUTS = 2 * SLICE
-ORDER = (0, 2, 1, 3)
+FIRST_PUT = 320
+SCALAR_PUTS = 704
+MASKINGS = ((0, 1024), (1024, 2048))
 MERGES = ((0, 256), (256, 640), (640, 1088), (1088, 1568), (1568, 2048))
 
 
@@ -35,6 +36,8 @@ def tile_picked_idxput_gate_e_kernel(tc, xT, mem, w1_words, w1_scales, offs, slo
         psum = ctx.enter_context(tc.psum_pool(name="psum", bufs=1))
 
         store = keep.tile([P, U], F32, name="store")
+        kept = keep.tile([P, U], F32, name="kept")
+        mask = keep.tile([P, U], F32, name="mask")
         side = keep.tile([P, U], F32, name="side")
         slot_sb = keep.tile([P, S // 16], U16, name="slot_sb")
         offs_sb = keep.tile([P, S // 16], U16, name="offs_sb")
@@ -45,32 +48,32 @@ def tile_picked_idxput_gate_e_kernel(tc, xT, mem, w1_words, w1_scales, offs, slo
         warm_out = keep.tile([P, 1], F32, name="warm_out")
         nc.vector.memset(warm_in[:], 0.0)
         nc.scalar.activation(warm_out[:], warm_in[:], SIGMOID)
+        nc.vector.memset(side[:, 0:SCALAR_PUTS], 0.0)
+        nc.vector.memset(mask[:], 1.0)
+        nc.vector.memset(side[:, SCALAR_PUTS:U], 0.0)
         nc.vector.memset(w_scales[:].bitcast(I32), 0)
-        nc.vector.memset(side[:], 0.0)
 
         x_rows = xT.rearrange("(z p t) c -> z t p c", z=PASSES, t=4)
-        nc.sync.dma_start(out=store[:], in_=mem)
         nc.sync.dma_start(slot_sb[:], slot)
         nc.sync.dma_start(offs_sb[:], offs)
-        for q in range(4):
-            nc.sync.dma_start(
-                out=w_scales[32 * q : 32 * q + 4, :, :].bitcast(I32),
-                in_=w1_scales[:, 4 * q : 4 * q + 4, :].rearrange("z r c -> r z c").bitcast(I32),
-            )
         rows = {}
         for z in range(PASSES):
             for t in range(4):
                 rows[z, t] = keep.tile([P, T], F32, name="row%d_%d" % (z, t), align_bytes=64)
                 nc.sync.dma_start(out=rows[z, t][:], in_=x_rows[z, t])
         nc.sync.dma_start(out=w_words[:].bitcast(I32), in_=w1_words.rearrange("z p c -> p z c").bitcast(I32))
+        for q in range(4):
+            nc.sync.dma_start(
+                out=w_scales[32 * q : 32 * q + 4, :, :].bitcast(I32),
+                in_=w1_scales[:, 4 * q : 4 * q + 4, :].rearrange("z r c -> r z c").bitcast(I32),
+            )
+        nc.sync.dma_start(out=store[:], in_=mem)
 
         def entries(index_tile, a, b):
             return index_tile[:, a // 16 : b // 16]
 
-        old = keep.tile([P, S], F32, name="old", align_bytes=64)
-        nc.scalar.activation(old[:, 0:512], store[:].indirect(entries(slot_sb, 0, 512)), COPY)
-        nc.vector.tensor_copy(old[:, 512:S], store[:].indirect(entries(slot_sb, 512, S)))
-        nc.vector.tensor_copy(store[:].indirect(entries(slot_sb, 0, SCALAR_PUTS)), side[:, 0:SCALAR_PUTS])
+        nc.scalar.activation(mask[:].indirect(entries(slot_sb, 0, SLICE)), side[:, 0:SLICE], COPY)
+        nc.vector.tensor_copy(mask[:].indirect(entries(slot_sb, SLICE, SCALAR_PUTS)), side[:, SLICE:SCALAR_PUTS])
 
         woven = [keep.tile([P, S, 4], BF16, name="woven%d" % z, align_bytes=64) for z in range(PASSES)]
         codes = [keep.tile([P, S], U32, name="codes%d" % z, align_bytes=64) for z in range(PASSES)]
@@ -100,15 +103,11 @@ def tile_picked_idxput_gate_e_kernel(tc, xT, mem, w1_words, w1_scales, offs, slo
                 out=codes[z][:, a:b].bitcast(FP8X4), scales=scales[z][:, a:b], in_=woven[z][:, a:b, :].rearrange("p n t -> p (n t)")
             )
 
-        gate = [keep.tile([P, SLICE], F32, name="gate%d" % s) for s in range(SLICES)]
-        fresh = {}
-
-        def squash(s, bank):
+        def project(s, acc):
             a, b = span(s)
-            acc = psum.tile([P, SLICE], F32, name="acc%d" % s, tag="bank%d" % bank)
             for z in range(PASSES):
                 nc.tensor.matmul_mx(
-                    out=acc[:],
+                    out=acc,
                     lhsT=w_words[:, z, :].bitcast(FP4X4),
                     lhsT_scale=w_scales[:, z, :],
                     rhs=codes[z][:, a:b].bitcast(FP8X4),
@@ -116,19 +115,6 @@ def tile_picked_idxput_gate_e_kernel(tc, xT, mem, w1_words, w1_scales, offs, slo
                     start=(z == 0),
                     stop=(z == PASSES - 1),
                 )
-            nc.scalar.activation(gate[s][:], acc[:], SIGMOID)
-
-        def renew(s):
-            a, b = span(s)
-            fresh[s] = keep.tile([P, SLICE], F32, name="fresh%d" % s)
-            nc.vector.tensor_tensor(fresh[s][:], old[:, a:b], gate[s][:], MULT)
-
-        def put(s):
-            a, b = span(s)
-            if a < SCALAR_PUTS:
-                nc.scalar.activation(side[:].indirect(entries(slot_sb, a, b)), fresh[s][:], COPY)
-            else:
-                nc.vector.tensor_tensor(store[:].indirect(entries(slot_sb, a, b)), old[:, a:b], gate[s][:], MULT)
 
         rest = (SLICE, S)
         for z, u in ((0, 0), (0, 1), (1, 0)):
@@ -139,26 +125,42 @@ def tile_picked_idxput_gate_e_kernel(tc, xT, mem, w1_words, w1_scales, offs, slo
                 quantise(z, 0, S)
         gather(1, 2, [rest])
 
-        first, second, third, last = ORDER
-        gather(1, 3, [span(s) for s in (second, third, last)])
-        place(1, 1, *span(second))
-        quantise(1, *span(first))
-        place(1, 1, *span(third))
-        quantise(1, *span(second))
-        quantise(1, *span(third))
-        place(1, 1, *span(last))
-        for bank, s in enumerate((first, second, third)):
-            squash(s, bank)
-        renew(first)
-        quantise(1, *span(last))
-        put(first)
-        squash(last, 2)
-        put(second)
-        renew(third)
-        put(third)
-        put(last)
+        gather(1, 3, [span(s) for s in range(1, SLICES)])
+        place(1, 1, *span(1))
+        quantise(1, *span(0))
+        place(1, 1, *span(2))
+        quantise(1, *span(1))
+        place(1, 1, *span(3))
+        quantise(1, *span(2))
+        quantise(1, *span(3))
+        gates = keep.tile([P, SCALAR_PUTS], F32, name="gates")
+        for s in range(2):
+            a, b = span(s)
+            acc = psum.tile([P, SLICE], F32, name="acc%d" % s)
+            project(s, acc[:])
+            nc.scalar.activation(gates[:, a:b], acc[:], SIGMOID)
+        half = S // 2
+        shared = psum.tile([P, half], F32, name="shared")
+        project(2, shared[:, 0:SLICE])
+        nc.scalar.activation(gates[:, half:SCALAR_PUTS], shared[:, 0 : SCALAR_PUTS - half], SIGMOID)
+        project(3, shared[:, SLICE:half])
+
+        def put(a, b, tag):
+            fresh = keep.tile([P, b - a], F32, name="fresh%d" % a, tag=tag)
+            nc.vector.tensor_tensor(fresh[:], store[:].indirect(entries(slot_sb, a, b)), gates[:, a:b], MULT)
+            nc.scalar.activation(side[:].indirect(entries(slot_sb, a, b)), fresh[:], COPY)
+
+        old = keep.tile([P, S - SCALAR_PUTS], F32, name="old")
+        nc.scalar.activation(old[:], store[:].indirect(entries(slot_sb, SCALAR_PUTS, S)), COPY)
+        put(0, FIRST_PUT, "first")
+        last_gates = keep.tile([P, S - SCALAR_PUTS], F32, name="last_gates", tag="first")
+        nc.scalar.activation(last_gates[:], shared[:, SCALAR_PUTS - half : half], SIGMOID)
+        put(FIRST_PUT, SCALAR_PUTS, "second")
+        for a, b in MASKINGS:
+            nc.vector.tensor_tensor(kept[:, a:b], store[:, a:b], mask[:, a:b], MULT)
+        nc.vector.tensor_tensor(kept[:].indirect(entries(slot_sb, SCALAR_PUTS, S)), old[:], last_gates[:], MULT)
 
         for a, b in MERGES:
             merged = keep.tile([P, b - a], F32, name="merged%d" % a)
-            nc.vector.tensor_tensor(merged[:], store[:, a:b], side[:, a:b], ADD)
+            nc.vector.tensor_tensor(merged[:], kept[:, a:b], side[:, a:b], ADD)
             nc.sync.dma_start(out=out[:, a:b], in_=merged[:])

@@ -23,9 +23,9 @@ PASSES = K // 512
 
 SLICE = 256
 SLICES = S // SLICE
-FIRST_PUT = 320
-SCALAR_PUTS = 704
-MASKINGS = ((0, 1024), (1024, 2048))
+HALF = S // 2
+MEM_CUT = 1536
+MASKINGS = ((0, 768), (768, 1536), (1536, 2048))
 MERGES = ((0, 256), (256, 640), (640, 1088), (1088, 1568), (1568, 2048))
 
 
@@ -48,32 +48,32 @@ def tile_picked_idxput_gate_e_kernel(tc, xT, mem, w1_words, w1_scales, offs, slo
         warm_out = keep.tile([P, 1], F32, name="warm_out")
         nc.vector.memset(warm_in[:], 0.0)
         nc.scalar.activation(warm_out[:], warm_in[:], SIGMOID)
-        nc.vector.memset(side[:, 0:SCALAR_PUTS], 0.0)
-        nc.vector.memset(mask[:], 1.0)
-        nc.vector.memset(side[:, SCALAR_PUTS:U], 0.0)
         nc.vector.memset(w_scales[:].bitcast(I32), 0)
+        nc.vector.memset(mask[:], 1.0)
+        nc.vector.memset(side[:], 0.0)
 
         x_rows = xT.rearrange("(z p t) c -> z t p c", z=PASSES, t=4)
         nc.sync.dma_start(slot_sb[:], slot)
-        nc.sync.dma_start(offs_sb[:], offs)
         rows = {}
         for z in range(PASSES):
             for t in range(4):
                 rows[z, t] = keep.tile([P, T], F32, name="row%d_%d" % (z, t), align_bytes=64)
                 nc.sync.dma_start(out=rows[z, t][:], in_=x_rows[z, t])
+                if (z, t) == (0, 0):
+                    nc.sync.dma_start(offs_sb[:], offs)
+                    for q in range(4):
+                        nc.sync.dma_start(
+                            out=w_scales[32 * q : 32 * q + 4, :, :].bitcast(I32),
+                            in_=w1_scales[:, 4 * q : 4 * q + 4, :].rearrange("z r c -> r z c").bitcast(I32),
+                        )
+        nc.sync.dma_start(out=store[:, 0 : MEM_CUT], in_=mem[:, 0 : MEM_CUT])
         nc.sync.dma_start(out=w_words[:].bitcast(I32), in_=w1_words.rearrange("z p c -> p z c").bitcast(I32))
-        for q in range(4):
-            nc.sync.dma_start(
-                out=w_scales[32 * q : 32 * q + 4, :, :].bitcast(I32),
-                in_=w1_scales[:, 4 * q : 4 * q + 4, :].rearrange("z r c -> r z c").bitcast(I32),
-            )
-        nc.sync.dma_start(out=store[:], in_=mem)
+        nc.sync.dma_start(out=store[:, MEM_CUT : U], in_=mem[:, MEM_CUT : U])
 
         def entries(index_tile, a, b):
             return index_tile[:, a // 16 : b // 16]
 
-        nc.scalar.activation(mask[:].indirect(entries(slot_sb, 0, SLICE)), side[:, 0:SLICE], COPY)
-        nc.vector.tensor_copy(mask[:].indirect(entries(slot_sb, SLICE, SCALAR_PUTS)), side[:, SLICE:SCALAR_PUTS])
+        nc.vector.tensor_copy(mask[:].indirect(entries(slot_sb, 0, HALF)), side[:, 0:HALF])
 
         woven = [keep.tile([P, S, 4], BF16, name="woven%d" % z, align_bytes=64) for z in range(PASSES)]
         codes = [keep.tile([P, S], U32, name="codes%d" % z, align_bytes=64) for z in range(PASSES)]
@@ -103,11 +103,11 @@ def tile_picked_idxput_gate_e_kernel(tc, xT, mem, w1_words, w1_scales, offs, slo
                 out=codes[z][:, a:b].bitcast(FP8X4), scales=scales[z][:, a:b], in_=woven[z][:, a:b, :].rearrange("p n t -> p (n t)")
             )
 
-        def project(s, acc):
-            a, b = span(s)
+        def squash(a, b):
+            acc = psum.tile([P, b - a], F32, name="acc%d" % a)
             for z in range(PASSES):
                 nc.tensor.matmul_mx(
-                    out=acc,
+                    out=acc[:],
                     lhsT=w_words[:, z, :].bitcast(FP4X4),
                     lhsT_scale=w_scales[:, z, :],
                     rhs=codes[z][:, a:b].bitcast(FP8X4),
@@ -115,6 +115,7 @@ def tile_picked_idxput_gate_e_kernel(tc, xT, mem, w1_words, w1_scales, offs, slo
                     start=(z == 0),
                     stop=(z == PASSES - 1),
                 )
+            nc.scalar.activation(gates[:, a:b], acc[:], SIGMOID)
 
         rest = (SLICE, S)
         for z, u in ((0, 0), (0, 1), (1, 0)):
@@ -133,32 +134,20 @@ def tile_picked_idxput_gate_e_kernel(tc, xT, mem, w1_words, w1_scales, offs, slo
         place(1, 1, *span(3))
         quantise(1, *span(2))
         quantise(1, *span(3))
-        gates = keep.tile([P, SCALAR_PUTS], F32, name="gates")
-        for s in range(2):
-            a, b = span(s)
-            acc = psum.tile([P, SLICE], F32, name="acc%d" % s)
-            project(s, acc[:])
-            nc.scalar.activation(gates[:, a:b], acc[:], SIGMOID)
-        half = S // 2
-        shared = psum.tile([P, half], F32, name="shared")
-        project(2, shared[:, 0:SLICE])
-        nc.scalar.activation(gates[:, half:SCALAR_PUTS], shared[:, 0 : SCALAR_PUTS - half], SIGMOID)
-        project(3, shared[:, SLICE:half])
-
-        def put(a, b, tag):
-            fresh = keep.tile([P, b - a], F32, name="fresh%d" % a, tag=tag)
-            nc.vector.tensor_tensor(fresh[:], store[:].indirect(entries(slot_sb, a, b)), gates[:, a:b], MULT)
-            nc.scalar.activation(side[:].indirect(entries(slot_sb, a, b)), fresh[:], COPY)
-
-        old = keep.tile([P, S - SCALAR_PUTS], F32, name="old")
-        nc.scalar.activation(old[:], store[:].indirect(entries(slot_sb, SCALAR_PUTS, S)), COPY)
-        put(0, FIRST_PUT, "first")
-        last_gates = keep.tile([P, S - SCALAR_PUTS], F32, name="last_gates", tag="first")
-        nc.scalar.activation(last_gates[:], shared[:, SCALAR_PUTS - half : half], SIGMOID)
-        put(FIRST_PUT, SCALAR_PUTS, "second")
+        gates = keep.tile([P, S], F32, name="gates")
+        old = keep.tile([P, S], F32, name="old")
+        fresh = keep.tile([P, HALF], F32, name="fresh")
+        for a, b in (span(0), span(1), (HALF, S)):
+            nc.scalar.activation(old[:, a:b], store[:].indirect(entries(slot_sb, a, b)), COPY)
+            squash(a, b)
+        for a, b in (span(0), span(1)):
+            nc.vector.tensor_tensor(fresh[:, a:b], old[:, a:b], gates[:, a:b], MULT)
         for a, b in MASKINGS:
             nc.vector.tensor_tensor(kept[:, a:b], store[:, a:b], mask[:, a:b], MULT)
-        nc.vector.tensor_tensor(kept[:].indirect(entries(slot_sb, SCALAR_PUTS, S)), old[:], last_gates[:], MULT)
+        for s in range(2):
+            a, b = span(s)
+            nc.scalar.activation(side[:].indirect(entries(slot_sb, a, b)), fresh[:, a:b], COPY)
+        nc.vector.tensor_tensor(kept[:].indirect(entries(slot_sb, HALF, S)), old[:, HALF:S], gates[:, HALF:S], MULT)
 
         for a, b in MERGES:
             merged = keep.tile([P, b - a], F32, name="merged%d" % a)

@@ -24,7 +24,6 @@ PASSES = K // 512
 SLICE = 256
 SLICES = S // SLICE
 HALF = S // 2
-MEM_CUT = 1536
 MASKINGS = ((0, 768), (768, 1536), (1536, 2048))
 MERGES = ((0, 256), (256, 640), (640, 1088), (1088, 1568), (1568, 2048))
 
@@ -66,9 +65,8 @@ def tile_picked_idxput_gate_e_kernel(tc, xT, mem, w1_words, w1_scales, offs, slo
                             out=w_scales[32 * q : 32 * q + 4, :, :].bitcast(I32),
                             in_=w1_scales[:, 4 * q : 4 * q + 4, :].rearrange("z r c -> r z c").bitcast(I32),
                         )
-        nc.sync.dma_start(out=store[:, 0 : MEM_CUT], in_=mem[:, 0 : MEM_CUT])
         nc.sync.dma_start(out=w_words[:].bitcast(I32), in_=w1_words.rearrange("z p c -> p z c").bitcast(I32))
-        nc.sync.dma_start(out=store[:, MEM_CUT : U], in_=mem[:, MEM_CUT : U])
+        nc.sync.dma_start(out=store[:], in_=mem)
 
         def entries(index_tile, a, b):
             return index_tile[:, a // 16 : b // 16]
@@ -103,19 +101,20 @@ def tile_picked_idxput_gate_e_kernel(tc, xT, mem, w1_words, w1_scales, offs, slo
                 out=codes[z][:, a:b].bitcast(FP8X4), scales=scales[z][:, a:b], in_=woven[z][:, a:b, :].rearrange("p n t -> p (n t)")
             )
 
-        def squash(a, b):
-            acc = psum.tile([P, b - a], F32, name="acc%d" % a)
-            for z in range(PASSES):
-                nc.tensor.matmul_mx(
-                    out=acc[:],
-                    lhsT=w_words[:, z, :].bitcast(FP4X4),
-                    lhsT_scale=w_scales[:, z, :],
-                    rhs=codes[z][:, a:b].bitcast(FP8X4),
-                    rhs_scale=scales[z][:, a:b],
-                    start=(z == 0),
-                    stop=(z == PASSES - 1),
-                )
-            nc.scalar.activation(gates[:, a:b], acc[:], SIGMOID)
+        acc = {}
+
+        def multiply(z, a, b):
+            if z == 0:
+                acc[a] = psum.tile([P, b - a], F32, name="acc%d" % a)
+            nc.tensor.matmul_mx(
+                out=acc[a][:],
+                lhsT=w_words[:, z, :].bitcast(FP4X4),
+                lhsT_scale=w_scales[:, z, :],
+                rhs=codes[z][:, a:b].bitcast(FP8X4),
+                rhs_scale=scales[z][:, a:b],
+                start=(z == 0),
+                stop=(z == PASSES - 1),
+            )
 
         rest = (SLICE, S)
         for z, u in ((0, 0), (0, 1), (1, 0)):
@@ -134,20 +133,36 @@ def tile_picked_idxput_gate_e_kernel(tc, xT, mem, w1_words, w1_scales, offs, slo
         place(1, 1, *span(3))
         quantise(1, *span(2))
         quantise(1, *span(3))
-        gates = keep.tile([P, S], F32, name="gates")
-        old = keep.tile([P, S], F32, name="old")
+        first_gates = keep.tile([P, SLICE], F32, name="first_gates")
+        late_gates = keep.tile([P, S - SLICE], F32, name="late_gates")
         fresh = keep.tile([P, HALF], F32, name="fresh")
-        for a, b in (span(0), span(1), (HALF, S)):
-            nc.scalar.activation(old[:, a:b], store[:].indirect(entries(slot_sb, a, b)), COPY)
-            squash(a, b)
-        for a, b in (span(0), span(1)):
-            nc.vector.tensor_tensor(fresh[:, a:b], old[:, a:b], gates[:, a:b], MULT)
+        gates = {span(0): first_gates[:], span(1): late_gates[:, 0:SLICE], (HALF, S): late_gates[:, SLICE : S - SLICE]}
+        old = {
+            span(0): late_gates[:, SLICE // 2 : SLICE // 2 + SLICE],
+            span(1): keep.tile([P, SLICE], F32, name="old_second")[:],
+            (HALF, S): keep.tile([P, HALF], F32, name="old_late")[:],
+        }
+
+        def squash(a, b):
+            for z in range(PASSES):
+                multiply(z, a, b)
+            nc.scalar.activation(gates[a, b], acc[a][:], SIGMOID)
+
+        def renew(a, b):
+            nc.vector.tensor_tensor(fresh[:, a:b], old[a, b], gates[a, b], MULT)
+
+        squash(*span(0))
+        for a, b in old:
+            nc.scalar.activation(old[a, b], store[:].indirect(entries(slot_sb, a, b)), COPY)
+        renew(*span(0))
+        squash(*span(1))
+        squash(HALF, S)
         for a, b in MASKINGS:
             nc.vector.tensor_tensor(kept[:, a:b], store[:, a:b], mask[:, a:b], MULT)
-        for s in range(2):
-            a, b = span(s)
+        renew(*span(1))
+        for a, b in (span(0), span(1)):
             nc.scalar.activation(side[:].indirect(entries(slot_sb, a, b)), fresh[:, a:b], COPY)
-        nc.vector.tensor_tensor(kept[:].indirect(entries(slot_sb, HALF, S)), old[:, HALF:S], gates[:, HALF:S], MULT)
+        nc.vector.tensor_tensor(kept[:].indirect(entries(slot_sb, HALF, S)), old[HALF, S], gates[HALF, S], MULT)
 
         for a, b in MERGES:
             merged = keep.tile([P, b - a], F32, name="merged%d" % a)

@@ -23,7 +23,7 @@ PASSES = K // 512
 
 SLICE = 256
 SLICES = S // SLICE
-HALF = S // 2
+FIRST, SECOND, THIRD = (0, 256), (256, 576), (576, S)
 MASKINGS = ((0, 768), (768, 1536), (1536, 2048))
 MERGES = ((0, 256), (256, 640), (640, 1088), (1088, 1568), (1568, 2048))
 
@@ -71,7 +71,7 @@ def tile_picked_idxput_gate_e_kernel(tc, xT, mem, w1_words, w1_scales, offs, slo
         def entries(index_tile, a, b):
             return index_tile[:, a // 16 : b // 16]
 
-        nc.vector.tensor_copy(mask[:].indirect(entries(slot_sb, 0, HALF)), side[:, 0:HALF])
+        nc.vector.tensor_copy(mask[:].indirect(entries(slot_sb, 0, THIRD[0])), side[:, 0 : THIRD[0]])
 
         woven = [keep.tile([P, S, 4], BF16, name="woven%d" % z, align_bytes=64) for z in range(PASSES)]
         codes = [keep.tile([P, S], U32, name="codes%d" % z, align_bytes=64) for z in range(PASSES)]
@@ -101,21 +101,6 @@ def tile_picked_idxput_gate_e_kernel(tc, xT, mem, w1_words, w1_scales, offs, slo
                 out=codes[z][:, a:b].bitcast(FP8X4), scales=scales[z][:, a:b], in_=woven[z][:, a:b, :].rearrange("p n t -> p (n t)")
             )
 
-        acc = {}
-
-        def multiply(z, a, b):
-            if z == 0:
-                acc[a] = psum.tile([P, b - a], F32, name="acc%d" % a)
-            nc.tensor.matmul_mx(
-                out=acc[a][:],
-                lhsT=w_words[:, z, :].bitcast(FP4X4),
-                lhsT_scale=w_scales[:, z, :],
-                rhs=codes[z][:, a:b].bitcast(FP8X4),
-                rhs_scale=scales[z][:, a:b],
-                start=(z == 0),
-                stop=(z == PASSES - 1),
-            )
-
         rest = (SLICE, S)
         for z, u in ((0, 0), (0, 1), (1, 0)):
             gather(z, 2 * u, [rest])
@@ -135,34 +120,40 @@ def tile_picked_idxput_gate_e_kernel(tc, xT, mem, w1_words, w1_scales, offs, slo
         quantise(1, *span(3))
         first_gates = keep.tile([P, SLICE], F32, name="first_gates")
         late_gates = keep.tile([P, S - SLICE], F32, name="late_gates")
-        fresh = keep.tile([P, HALF], F32, name="fresh")
-        gates = {span(0): first_gates[:], span(1): late_gates[:, 0:SLICE], (HALF, S): late_gates[:, SLICE : S - SLICE]}
-        old = {
-            span(0): late_gates[:, SLICE // 2 : SLICE // 2 + SLICE],
-            span(1): keep.tile([P, SLICE], F32, name="old_second")[:],
-            (HALF, S): keep.tile([P, HALF], F32, name="old_late")[:],
-        }
+        fresh = keep.tile([P, THIRD[0]], F32, name="fresh")
+        late_old = keep.tile([P, S - SLICE], F32, name="late_old")
+        border = 2 * SLICE
+        first_old = late_gates[:, border - SLICE // 2 : border + SLICE // 2]
 
-        def squash(a, b):
+        def late(tile, part):
+            return tile[:, part[0] - SLICE : part[1] - SLICE]
+
+        def squash(a, b, gates):
+            acc = psum.tile([P, b - a], F32, name="acc%d" % a)
             for z in range(PASSES):
-                multiply(z, a, b)
-            nc.scalar.activation(gates[a, b], acc[a][:], SIGMOID)
+                nc.tensor.matmul_mx(
+                    out=acc[:],
+                    lhsT=w_words[:, z, :].bitcast(FP4X4),
+                    lhsT_scale=w_scales[:, z, :],
+                    rhs=codes[z][:, a:b].bitcast(FP8X4),
+                    rhs_scale=scales[z][:, a:b],
+                    start=(z == 0),
+                    stop=(z == PASSES - 1),
+                )
+            nc.scalar.activation(gates, acc[:], SIGMOID)
 
-        def renew(a, b):
-            nc.vector.tensor_tensor(fresh[:, a:b], old[a, b], gates[a, b], MULT)
-
-        squash(*span(0))
-        for a, b in old:
-            nc.scalar.activation(old[a, b], store[:].indirect(entries(slot_sb, a, b)), COPY)
-        renew(*span(0))
-        squash(*span(1))
-        squash(HALF, S)
+        squash(0, SLICE, first_gates[:])
+        nc.scalar.activation(first_old, store[:].indirect(entries(slot_sb, *FIRST)), COPY)
+        nc.scalar.activation(late_old[:], store[:].indirect(entries(slot_sb, SLICE, S)), COPY)
+        nc.vector.tensor_tensor(fresh[:, 0:SLICE], first_old, first_gates[:], MULT)
+        squash(SLICE, SLICE + border, late_gates[:, 0:border])
+        squash(SLICE + border, S, late_gates[:, border : S - SLICE])
         for a, b in MASKINGS:
             nc.vector.tensor_tensor(kept[:, a:b], store[:, a:b], mask[:, a:b], MULT)
-        renew(*span(1))
-        for a, b in (span(0), span(1)):
+        nc.vector.tensor_tensor(fresh[:, SECOND[0] : SECOND[1]], late(late_old, SECOND), late(late_gates, SECOND), MULT)
+        for a, b in (FIRST, SECOND):
             nc.scalar.activation(side[:].indirect(entries(slot_sb, a, b)), fresh[:, a:b], COPY)
-        nc.vector.tensor_tensor(kept[:].indirect(entries(slot_sb, HALF, S)), old[HALF, S], gates[HALF, S], MULT)
+        nc.vector.tensor_tensor(kept[:].indirect(entries(slot_sb, *THIRD)), late(late_old, THIRD), late(late_gates, THIRD), MULT)
 
         for a, b in MERGES:
             merged = keep.tile([P, b - a], F32, name="merged%d" % a)

@@ -23,7 +23,7 @@ PASSES = K // 512
 
 SLICE = 256
 SLICES = S // SLICE
-FIRST, SECOND, THIRD = (0, 256), (256, 576), (576, S)
+FIRST, SECOND, THIRD = (0, 256), (256, 544), (544, S)
 MASKINGS = ((0, 768), (768, 1536), (1536, 2048))
 MERGES = ((0, 256), (256, 640), (640, 1088), (1088, 1568), (1568, 2048))
 

@@ -48,8 +48,9 @@ def tile_picked_idxput_gate_e_kernel(tc, xT, mem, w1_words, w1_scales, offs, slo
         nc.vector.memset(warm_in[:], 0.0)
         nc.scalar.activation(warm_out[:], warm_in[:], SIGMOID)
         nc.vector.memset(w_scales[:].bitcast(I32), 0)
+        nc.vector.memset(side[:, 0 : THIRD[0]], 0.0)
         nc.vector.memset(mask[:], 1.0)
-        nc.vector.memset(side[:], 0.0)
+        nc.vector.memset(side[:, THIRD[0] : U], 0.0)
 
         x_rows = xT.rearrange("(z p t) c -> z t p c", z=PASSES, t=4)
         nc.sync.dma_start(slot_sb[:], slot)
@@ -71,7 +72,8 @@ def tile_picked_idxput_gate_e_kernel(tc, xT, mem, w1_words, w1_scales, offs, slo
         def entries(index_tile, a, b):
             return index_tile[:, a // 16 : b // 16]
 
-        nc.vector.tensor_copy(mask[:].indirect(entries(slot_sb, 0, THIRD[0])), side[:, 0 : THIRD[0]])
+        nc.scalar.activation(mask[:].indirect(entries(slot_sb, *FIRST)), side[:, FIRST[0] : FIRST[1]], COPY)
+        nc.vector.tensor_copy(mask[:].indirect(entries(slot_sb, *SECOND)), side[:, SECOND[0] : SECOND[1]])
 
         woven = [keep.tile([P, S, 4], BF16, name="woven%d" % z, align_bytes=64) for z in range(PASSES)]
         codes = [keep.tile([P, S], U32, name="codes%d" % z, align_bytes=64) for z in range(PASSES)]

from contextlib import ExitStack

import concourse.mybir as mybir

K, T, S, N, U = 1024, 2048, 1024, 128, 2048
FLOPS = 2 * K * N * S

F32 = mybir.dt.float32
BF16 = mybir.dt.bfloat16
U32 = mybir.dt.uint32
I32 = mybir.dt.int32
U16 = mybir.dt.uint16
U8 = mybir.dt.uint8
FP8X4 = mybir.dt.float8_e4m3fn_x4
FP4X4 = mybir.dt.float4_e2m1fn_x4
SIGMOID = mybir.ActivationFunctionType.Sigmoid
COPY = mybir.ActivationFunctionType.Copy
MULT = mybir.AluOpType.mult
ADD = mybir.AluOpType.add

P = 128
PASSES = K // 512

SLICE = 256
SLICES = S // SLICE
FIRST, SECOND, THIRD = (0, 256), (256, 544), (544, S)
MASKINGS = ((0, 768), (768, 1536), (1536, 2048))
MERGES = ((0, 256), (256, 640), (640, 1088), (1088, 1568), (1568, 2048))


def tile_picked_idxput_gate_e_kernel(tc, xT, mem, w1_words, w1_scales, offs, slot, out):
    nc = tc.nc
    with ExitStack() as ctx:
        keep = ctx.enter_context(tc.tile_pool(name="keep", bufs=1))
        psum = ctx.enter_context(tc.psum_pool(name="psum", bufs=1))

        store = keep.tile([P, U], F32, name="store")
        kept = keep.tile([P, U], F32, name="kept")
        mask = keep.tile([P, U], F32, name="mask")
        side = keep.tile([P, U], F32, name="side")
        slot_sb = keep.tile([P, S // 16], U16, name="slot_sb")
        offs_sb = keep.tile([P, S // 16], U16, name="offs_sb")
        w_words = keep.tile([P, PASSES, 2 * N], U8, name="w_words", align_bytes=64)
        w_scales = keep.tile([P, PASSES, N], U8, name="w_scales", align_bytes=64)

        warm_in = keep.tile([P, 1], F32, name="warm_in")
        warm_out = keep.tile([P, 1], F32, name="warm_out")
        nc.vector.memset(warm_in[:], 0.0)
        nc.scalar.activation(warm_out[:], warm_in[:], SIGMOID)
        nc.vector.memset(w_scales[:].bitcast(I32), 0)
        nc.vector.memset(side[:, 0 : THIRD[0]], 0.0)
        nc.vector.memset(mask[:], 1.0)
        nc.vector.memset(side[:, THIRD[0] : U], 0.0)

        x_rows = xT.rearrange("(z p t) c -> z t p c", z=PASSES, t=4)
        nc.sync.dma_start(slot_sb[:], slot)
        rows = {}
        for z in range(PASSES):
            for t in range(4):
                rows[z, t] = keep.tile([P, T], F32, name="row%d_%d" % (z, t), align_bytes=64)
                nc.sync.dma_start(out=rows[z, t][:], in_=x_rows[z, t])
                if (z, t) == (0, 0):
                    nc.sync.dma_start(offs_sb[:], offs)
                    for q in range(4):
                        nc.sync.dma_start(
                            out=w_scales[32 * q : 32 * q + 4, :, :].bitcast(I32),
                            in_=w1_scales[:, 4 * q : 4 * q + 4, :].rearrange("z r c -> r z c").bitcast(I32),
                        )
        nc.sync.dma_start(out=w_words[:].bitcast(I32), in_=w1_words.rearrange("z p c -> p z c").bitcast(I32))
        nc.sync.dma_start(out=store[:], in_=mem)

        def entries(index_tile, a, b):
            return index_tile[:, a // 16 : b // 16]

        nc.scalar.activation(mask[:].indirect(entries(slot_sb, *FIRST)), side[:, FIRST[0] : FIRST[1]], COPY)
        nc.vector.tensor_copy(mask[:].indirect(entries(slot_sb, *SECOND)), side[:, SECOND[0] : SECOND[1]])

        woven = [keep.tile([P, S, 4], BF16, name="woven%d" % z, align_bytes=64) for z in range(PASSES)]
        codes = [keep.tile([P, S], U32, name="codes%d" % z, align_bytes=64) for z in range(PASSES)]
        scales = [keep.tile([P, S], U8, name="scales%d" % z, align_bytes=64) for z in range(PASSES)]
        planes = {}
        for z in range(PASSES):
            for u in range(2):
                planes[z, u] = keep.tile([P, 2, S - SLICE], BF16, name="planes%d_%d" % (z, u), align_bytes=64)

        def span(s):
            return s * SLICE, (s + 1) * SLICE

        def gather(z, t, spans):
            nc.vector.tensor_copy(woven[z][:, 0:SLICE, t], rows[z, t][:].indirect(entries(offs_sb, 0, SLICE)))
            for a, b in spans:
                nc.scalar.activation(
                    planes[z, t // 2][:, t % 2, a - SLICE : b - SLICE], rows[z, t][:].indirect(entries(offs_sb, a, b)), COPY
                )

        def place(z, u, a, b):
            nc.vector.tensor_copy(
                woven[z][:, a:b, 2 * u : 2 * u + 2], planes[z, u][:, :, a - SLICE : b - SLICE].rearrange("p e n -> p n e")
            )

        def quantise(z, a, b):
            nc.vector.quantize_mx(
                out=codes[z][:, a:b].bitcast(FP8X4), scales=scales[z][:, a:b], in_=woven[z][:, a:b, :].rearrange("p n t -> p (n t)")
            )

        rest = (SLICE, S)
        for z, u in ((0, 0), (0, 1), (1, 0)):
            gather(z, 2 * u, [rest])
            gather(z, 2 * u + 1, [rest])
            place(z, u, *rest)
            if u == 1:
                quantise(z, 0, S)
        gather(1, 2, [rest])

        gather(1, 3, [span(s) for s in range(1, SLICES)])
        place(1, 1, *span(1))
        quantise(1, *span(0))
        place(1, 1, *span(2))
        quantise(1, *span(1))
        place(1, 1, *span(3))
        quantise(1, *span(2))
        quantise(1, *span(3))
        first_gates = keep.tile([P, SLICE], F32, name="first_gates")
        late_gates = keep.tile([P, S - SLICE], F32, name="late_gates")
        fresh = keep.tile([P, THIRD[0]], F32, name="fresh")
        late_old = keep.tile([P, S - SLICE], F32, name="late_old")
        border = 2 * SLICE
        first_old = late_gates[:, border - SLICE // 2 : border + SLICE // 2]

        def late(tile, part):
            return tile[:, part[0] - SLICE : part[1] - SLICE]

        def squash(a, b, gates):
            acc = psum.tile([P, b - a], F32, name="acc%d" % a)
            for z in range(PASSES):
                nc.tensor.matmul_mx(
                    out=acc[:],
                    lhsT=w_words[:, z, :].bitcast(FP4X4),
                    lhsT_scale=w_scales[:, z, :],
                    rhs=codes[z][:, a:b].bitcast(FP8X4),
                    rhs_scale=scales[z][:, a:b],
                    start=(z == 0),
                    stop=(z == PASSES - 1),
                )
            nc.scalar.activation(gates, acc[:], SIGMOID)

        squash(0, SLICE, first_gates[:])
        nc.scalar.activation(first_old, store[:].indirect(entries(slot_sb, *FIRST)), COPY)
        nc.scalar.activation(late_old[:], store[:].indirect(entries(slot_sb, SLICE, S)), COPY)
        nc.vector.tensor_tensor(fresh[:, 0:SLICE], first_old, first_gates[:], MULT)
        squash(SLICE, SLICE + border, late_gates[:, 0:border])
        squash(SLICE + border, S, late_gates[:, border : S - SLICE])
        for a, b in MASKINGS:
            nc.vector.tensor_tensor(kept[:, a:b], store[:, a:b], mask[:, a:b], MULT)
        nc.vector.tensor_tensor(fresh[:, SECOND[0] : SECOND[1]], late(late_old, SECOND), late(late_gates, SECOND), MULT)
        for a, b in (FIRST, SECOND):
            nc.scalar.activation(side[:].indirect(entries(slot_sb, a, b)), fresh[:, a:b], COPY)
        nc.vector.tensor_tensor(kept[:].indirect(entries(slot_sb, *THIRD)), late(late_old, THIRD), late(late_gates, THIRD), MULT)

        for a, b in MERGES:
            merged = keep.tile([P, b - a], F32, name="merged%d" % a)
            nc.vector.tensor_tensor(merged[:], kept[:, a:b], side[:, a:b], ADD)
            nc.sync.dma_start(out=out[:, a:b], in_=merged[:])
